import numpy as np, ml_dtypes
CORES = [48,51,52,55]
N = 4
BF = ml_dtypes.bfloat16
def gentries(a):
    return np.ascontiguousarray(a.reshape(8, 16, -1).transpose(0, 2, 1)).reshape(8, -1)
def gtable(e):
    e = np.asarray(e); return np.ascontiguousarray(e.reshape(8, -1, 16).transpose(0, 2, 1)).reshape(128, -1).astype(np.int32)
V, A, K, DB, DP, EP = 2560, 64, 4, 5, 32, 2
RI, GI, G8 = np.arange(N)[:, None, None], np.arange(8)[None, :, None], np.arange(8)[:, None]
def pick(a, i):
    return a[RI, GI, i]
def tall(x):
    return np.ascontiguousarray(x.astype(np.float32).reshape(N, 8, 16, V).transpose(0, 1, 3, 2)).astype(np.int32)
def depths(par):
    j = np.reshape(par, (-1, V)).astype(np.int64); t = np.zeros(j.shape, np.int64) + np.arange(V); n = np.zeros(j.shape, np.int64)
    for _ in range(DP):
        n += t >= A; t = np.take_along_axis(j, t, 1)
    return n.reshape(np.shape(par))
def forest(rng, m, power):
    n = V - A; lev = np.minimum(1 + np.floor(m * rng.random(n) ** power).astype(np.int64), m); lev[rng.permutation(n)[:m]] = np.arange(1, m + 1)
    p = np.arange(V); o = A + np.argsort(lev, kind="stable"); cnt = np.bincount(lev, minlength=m + 1); before = np.arange(A); a = 0
    for l in range(1, m + 1):
        now = o[a:a + cnt[l]]; p[now] = before[rng.integers(0, before.size, now.size)]; before = now; a += cnt[l]
    return p
def parts(rng, deep, power):
    hf = 1 - 2 * rng.integers(0, 2, (N, 128, V)); bt = rng.integers(0, 256, (N, 128, V)); dr = rng.integers(0, 256, (N, 128, V))
    par = np.stack([np.stack([forest(rng, int(deep[r, g]), float(power[r, g])) for g in range(8)]) for r in range(N)])
    return hf, bt, dr, par, rng.integers(0, V, (N, 8, K, V)), rng.integers(0, V, (N, 8, A))
def pack(hf, bt, dr, par, nb, up):
    return {"hf": hf.astype(np.float32).astype(BF), "bt": bt.astype(np.float32).astype(BF), "dr": dr.astype(np.float32).astype(BF), "par": par.astype(np.int32),
            "nb": np.stack([gtable(a.reshape(8, -1)) for a in nb]), "up": np.stack([gtable(a) for a in up])}
def setup_inputs(rng):
    deep = rng.choice(np.array([DP - 1, DP // 2 + 1, DP // 2, DP // 4]), (N, 8)); deep[:, rng.integers(0, 8)] = DP - 1; deep[0, 0] = DP - 1
    return pack(*parts(rng, deep, rng.choice(np.array([0.5, 1.0, 1.5]), (N, 8))))
def setup_inputs_deep(rng):
    hf, bt, dr, par, nb, up = parts(rng, np.full((N, 8), DP - 1), rng.choice(np.array([0.1, 0.25]), (N, 8)))
    o = np.argsort(-depths(par), axis=-1, kind="stable")[:, :, :A]
    for r in range(1, N): up[r] = rng.permuted(o[r - 1], axis=-1)
    hf[:, 16:32] = 1; hf[0, 16:24, :A] = -1; bt[:, 16:32] = 255; dr[:, 16:32] = 0; nb[:, 1] = np.arange(V)
    return pack(hf, bt, dr, par, nb, up)
def setup_inputs_ties(rng):
    hf, bt, dr, par, nb, up = parts(rng, rng.choice(np.array([DP - 1, DP // 2, 5]), (N, 8)), np.full((N, 8), 1.0))
    bt = (bt >> 6) * 64; dr = (dr >> 6) * 64; h4, b4, d4 = hf.reshape(N, 8, 16, V), bt.reshape(N, 8, 16, V), dr.reshape(N, 8, 16, V)
    h4[:, ::2] = h4[:, ::2, :1]; b4[:, ::2] = (b4[:, ::2, :1] >> 7) * 128; d4[:, ::2] = (d4[:, ::2, :1] >> 7) * 128
    nb[:, :, 1:] = np.where(rng.random((N, 8, K - 1, V)) < 0.2, nb[:, :, :1], nb[:, :, 1:]); nb = np.where(rng.random(nb.shape) < 0.1, np.arange(V), nb)
    return pack(hf, bt, dr, par, nb, up)
def setup_inputs_flat(rng):
    deep = np.full((N, 8), DP // 2); deep[:, 0] = 1; deep[:, 1] = 2; deep[:, 2] = DP - 1
    hf, bt, dr, par, nb, up = parts(rng, deep, np.full((N, 8), 1.0)); dep = depths(par); v = np.arange(V); hf[:, 64:80] = 1
    for r in range(N):
        par[r, 1] = np.where(dep[r, 1] == 2, np.flatnonzero(dep[r, 1] == 1)[0], par[r, 1])
        ch = np.arange(V); ch[par[r, 7, A:]] = np.arange(A, V); nb[r, 7, 0] = ch
        c = np.where(v < A, v, 2 * rng.integers(0, A // 2, V) + dep[r, 4] % 2); c = np.where((v >= A) & (c == par[r, 4]), (c + 2) % A, c)
        w = bt[r, 64:80, :A][:, c]; bt[r, 64:80, A:] = (w - w[:, par[r, 4]])[:, A:] & 255; nb[r, 4, r % K] = c
    nb[:, 2] = np.arange(V); hf[:, 48:64] = -1; bt[:, 48:64] = 255; dr[:, 48:64] = 255; up[:, 4] = V - 1; up[:, 5] = rng.integers(0, A, (N, A))
    up[:, 6] = rng.choice(np.array([0, V - 1]), (N, A)); nb[:, 6] = rng.choice(np.array([0, A - 1, A, V - 1]), (N, K, V))
    return pack(hf, bt, dr, par, nb, up)
def setup_inputs_spread(rng):
    hf, bt, dr, par, nb, up = parts(rng, rng.integers(1, DP, (N, 8)), rng.choice(np.array([0.2, 1.0, 4.0]), (N, 8)))
    share = rng.choice(np.array([0.02, 0.3, 0.5, 0.98]), (N, 8, 1, 1)); hf = np.where(rng.random((N, 8, 16, V)) < share, -1, 1).reshape(N, 128, V)
    k = lambda: rng.integers(0, 9, (N, 1, V)); bt = (bt >> k()) * (rng.random((N, 1, V)) > 0.0625); dr = (dr >> k()) * (rng.random((N, 1, V)) > 0.0625)
    nb = np.minimum((V * rng.random(nb.shape) ** 3).astype(np.int64), V - 1); up = np.minimum((V * rng.random(up.shape) ** 3).astype(np.int64), V - 1)
    return pack(hf, bt, dr, par, nb, up)
def check_inputs(d):
    bad = []
    if not np.all(np.abs(d["hf"].astype(np.float32)) == 1): bad.append("hf is 1 or -1")
    for k in ("bt", "dr"):
        x = d[k].astype(np.float32)
        if not np.all((x >= 0) & (x <= 255) & (x == np.floor(x))): bad.append("range of " + k)
    for k in ("par", "nb", "up"):
        if np.min(d[k]) < 0 or np.max(d[k]) > V - 1: bad.append("range of " + k)
    if "range of par" not in bad:
        if np.any(d["par"][:, :, :A] != np.arange(A)): bad.append("an anchor is its own parent")
        if np.max(depths(d["par"])) >= DP: bad.append("depth")
    return bad
def reference(hf, bt, dr, par, nb, up):
    h, b, d = tall(hf), tall(bt), tall(dr); g = np.where(d >= 128, -1, 1).astype(np.int32); move = np.arange(V) >= A
    p = par.astype(np.int64); nl = np.stack([gentries(a) for a in nb]).astype(np.int64).reshape(N, 8, K, V); ul = np.stack([gentries(a) for a in up]).astype(np.int64)
    for e in range(EP):
        Hm = h.copy(); Zm = b.copy(); Hm[:, :, :A] = 1; Zm[:, :, :A] = 0
        j = p; dep = np.broadcast_to(move, p.shape).astype(np.int64)
        for _ in range(DB):
            hp = pick(Hm, j); Zm = hp * Zm + pick(Zm, j); Hm = hp * Hm; dep = dep + pick(dep, j); j = pick(j, j)
        H = np.empty_like(Hm); Z = np.empty_like(Zm)
        for r in range(N):
            ah, az = h[r, :, :A], b[r, :, :A]
            if r > 0:
                uh = H[r - 1][G8, ul[r]]; az = uh * az + Z[r - 1][G8, ul[r]]; ah = uh * ah
            ch = ah[G8, j[r]]; H[r] = ch * Hm[r]; Z[r] = (ch * Zm[r] + az[G8, j[r]]) & 255
        best = np.add.reduce(np.abs(Z - pick(Z, p)), axis=3); new = p
        for k in range(K):
            c = pick(p, nl[:, :, k]); s = np.add.reduce(np.abs(Z - pick(Z, c)), axis=3)
            ok = (pick(dep, c) < dep) & (s < best)
            new = np.where(ok, c, new); best = np.where(ok, s, best)
        p = new
        if e < EP - 1:
            hp = pick(H, p); zb = (hp * (Z - pick(Z, p)) + d) & 255; m = move[:, None]
            h = np.where(m, g * hp * H, h); b = np.where(m, zb, b)
    return {"yx": np.ascontiguousarray(Z.transpose(0, 1, 3, 2)).reshape(N, 128, V).astype(np.float32).astype(BF), "yp": p.astype(np.float32)}

@@ -1,0 +1,557 @@
+from concourse.bass import DstId, RemoteDMATransfer
+from concourse.mybir import AluOpType as ALU, ActivationFunctionType as ACT
+
+V, A, NW = 2560, 64, 160
+CB = 34816.0
+P_ON_G, S_ON_G = (0, 2), (0, 2, 4)
+ZS, RS, KS = 1280, 1280, 1792
+
+SCRATCH = {}
+for _n in ("h", "b", "d", "gh", "av", "P0", "P1", "PD", "T1", "T2", "s", "ahr", "Z", "Zp", "tb", "D0", "D1", "D2", "U0", "U1"):
+    SCRATCH[_n] = ("sbuf", [128, V], "bfloat16")
+for _n in ("C0", "C1"):
+    SCRATCH[_n] = ("sbuf", [128, 5 * V], "bfloat16")
+for _n in ("S0", "S1", "SD"):
+    SCRATCH[_n] = ("sbuf", [128, V], "float32")
+for _n in range(6):
+    SCRATCH["L%d" % _n] = ("sbuf", [128, NW], "uint16")
+for _n in ("W0", "W1", "W2", "W3", "W4", "XA", "XB", "XC"):
+    SCRATCH["ps" + _n] = ("psum", [128, 512], "float32")
+for _n in ("I1", "Im1", "I2", "Im2", "I256", "I512", "I768", "Ih"):
+    SCRATCH[_n] = ("sbuf", [128, 128], "bfloat16")
+for _n in ("BE", "BD", "BD2", "BDm", "BF", "BFm"):
+    SCRATCH[_n] = ("sbuf", [128, 144], "bfloat16")
+SCRATCH.update({
+    "I32": ("sbuf", [128, 128], "float32"), "xi": ("sbuf", [128, 144], "float32"),
+    "ck": ("sbuf", [128, 5 * NW], "bfloat16"), "cc": ("sbuf", [128, 2 * NW], "bfloat16"),
+    "ki": ("sbuf", [128, 4], "int32"), "kj": ("sbuf", [128, 4], "int32"), "kf": ("sbuf", [128, 8], "float32"),
+    "pb": ("sbuf", [128, NW], "int32"), "pa": ("sbuf", [128, 2 * NW], "int32"), "hl": ("sbuf", [128, 2 * NW], "bfloat16"),
+    "nbi": ("sbuf", [128, 4 * NW], "int32"), "nbl": ("sbuf", [128, 4 * NW], "uint16"),
+    "upi": ("sbuf", [128, 4], "int32"), "upr": ("sbuf", [128, 4], "int32"), "upl": ("sbuf", [128, 4], "uint16"),
+    "l16": ("sbuf", [128, 4], "uint16"), "tu": ("sbuf", [128, A], "bfloat16"),
+    "absv": ("sbuf", [128, NW], "bfloat16"), "pen": ("sbuf", [128, 4 * NW], "bfloat16"),
+    "best": ("sbuf", [128, NW], "float32"), "bi": ("sbuf", [128, NW], "int32"), "bj": ("sbuf", [128, NW], "int32"),
+    "idx": ("sbuf", [128, NW], "uint16"), "po": ("sbuf", [128, NW], "float32"),
+    "ni": ("sbuf", [128, A], "int32"), "nj": ("sbuf", [128, A], "int32"),
+    "ah": ("sbuf", [128, A], "bfloat16"), "kz": ("sbuf", [128, A], "bfloat16"),
+})
+for _n in ("su", "x2", "xs", "xb", "xu", "z1", "z2", "kc", "ones"):
+    SCRATCH[_n] = ("sbuf", [128, A], "float32")
+for _e in range(2):
+    for _r in range(3):
+        SCRATCH["m%d%d" % (_e, _r)] = ("sbuf", [128, A], "bfloat16")
+        SCRATCH["n%d%d" % (_e, _r)] = ("sbuf", [128, A], "float32")
+        SCRATCH["r%d%d" % (_e, _r)] = ("sbuf", [128, A], "uint16")
+
+SEMAPHORES = ["cv", "ca", "ct", "cg", "sent", "upr"] + ["d%d" % _n for _n in range(90)] + \
+    ["%s%d%d" % (_k, _e, _r) for _k in "mnr" for _e in range(2) for _r in range(3)]
+
+
+def rank_program(g, core, T, topo):
+    r = T.rank_of(core)
+    if r is None:
+        return
+    NR = len(T.cores)
+    ops, acc, ndma, sent = [], {}, [0], [0]
+
+    def X(name, a=0, b=None, step=1, rows=None):
+        t = T[name]
+        b = t.shape[1] if b is None else b
+        if rows is not None:
+            ap = t[rows:128:16, a:b]
+        else:
+            ap = t[:, a:b] if step == 1 else t[:, a:b:step]
+        return (ap, [(name, a, b, rows)])
+
+    def G(win, off):
+        return (win[0].indirect(off[0]), win[1] + off[1])
+
+    def op(q, fn, outs, ins, sem=None, n=1):
+        me, deps = len(ops), set()
+        for wr, regs in ((False, ins), (True, outs)):
+            for x in regs:
+                if not isinstance(x, tuple):
+                    continue
+                for name, a, b, rows in x[1]:
+                    w = wr
+                    if name.startswith("ps"):
+                        a, b, w = 0, 512, True
+                    keep = []
+                    for (a2, b2, rows2, w2, j) in acc.get(name, []):
+                        hit = a < b2 and a2 < b and (rows is None or rows2 is None or rows == rows2)
+                        if hit and (w or w2) and j != me and not (q == "t" and ops[j]["q"] == "t"):
+                            deps.add(j)
+                        if not (w and rows is None and a <= a2 and b2 <= b):
+                            keep.append((a2, b2, rows2, w2, j))
+                    acc[name] = keep + [(a, b, rows, w, me)]
+        ops.append({"q": q, "fn": fn, "deps": deps, "sem": sem, "n": n})
+
+    def dma(q, out, in_):
+        k = ndma[0]
+        ndma[0] += 1
+        e = g.sync if q == "s" else g.scalar
+        op(q, lambda: e.dma_start(out[0], in_[0]), [out], [in_], sem="d%d" % k, n=16)
+
+    def dram(t):
+        return (t[:], [])
+
+    def tt(o, a, b, alu):
+        op("v", lambda: g.vector.tensor_tensor(o[0], a[0], b[0], alu), [o], [a, b])
+
+    def ts(o, a, s1, s2, o0, o1=None):
+        v1 = s1[0] if isinstance(s1, tuple) else s1
+        v2 = s2[0] if isinstance(s2, tuple) else s2
+        if o1 is None:
+            op("v", lambda: g.vector.tensor_scalar(o[0], a[0], v1, None, o0), [o], [a, s1])
+        else:
+            op("v", lambda: g.vector.tensor_scalar(o[0], a[0], v1, v2, o0, o1), [o], [a, s1, s2])
+
+    def cp(o, a):
+        op("v", lambda: g.vector.tensor_copy(o[0], a[0]), [o], [a])
+
+    def fill(o, c):
+        op("v", lambda: g.vector.memset(o[0], c), [o], [])
+
+    def act(o, a, f, bias=0.0, scale=1.0):
+        op("a", lambda: g.scalar.activation(o[0], a[0], f, bias=bias, scale=scale), [o], [a])
+
+    def mm(o, l, x, start, stop):
+        op("t", lambda: g.tensor.matmul(o[0], l[0], x[0], start, stop), [o], [l, x])
+
+    def wrap(bank, c0, n, src, col, base, start=True, stop=True):
+        for i in range(16):
+            mm(X(bank, c0, c0 + n), X(base, 15 - i, 143 - i), X(src, col + i, col + 16 * n, 16), start and i == 0, stop and i == 15)
+
+    def later(k):
+        return list(range(k + 1, NR))
+
+    def engines(k, dsts, part):
+        es = [e for e in topo.engines(T.cores[k], T.cores[dsts[0]]) if all(e in topo.engines(T.cores[k], T.cores[x]) for x in dsts)]
+        return es if part is None else es[part * len(es) // 2:(part + 1) * len(es) // 2]
+
+    def part_of(kind, k):
+        if kind == "r":
+            return 1
+        return 0 if kind == "m" or k == 0 else None
+
+    def send(items, dsts):
+        ids = [DstId(rid=topo.addr(T.cores[k])[0], pnc=topo.addr(T.cores[k])[1]) for k in dsts]
+        tr = []
+        for src, land, part in items:
+            es = engines(r, dsts, part)
+            sent[0] += len(es)
+            tr.append(RemoteDMATransfer(dst_ids=ids, dma_engine_mask=sum(1 << e for e in es), remote_sem=T.sem[land],
+                                        srcs=[T[src][:]], dsts=[T[land][:] for _ in dsts]))
+        op("g", lambda: g.remote_dma_fused(tr, local_sem=T.sem.sent), [], [X(x[0]) for x in items], sem="")
+
+    def arrive(name, frm, dsts, part):
+        op("x", None, [X(name)], [], sem=name, n=len(engines(frm, dsts, part)))
+
+    H = V // 2
+    BK = [(512 * j, 512 * j + 512) for j in range(5)]
+    WB = ["psW%d" % j for j in range(5)]
+    XB3 = ["psXA", "psXB", "psXC"]
+    PT = [(0, 1024), (1024, V)]
+    KB = {0: ("psXA", 0), 1: ("psXA", NW), 2: ("psXB", 0), 3: ("psXB", NW), 4: ("psXC", 0)}
+
+    def kf(j):
+        return X("kf", j, j + 1)
+
+    def mklist(part, src):
+        a, b = PT[part]
+        wrap(XB3[part], 0, (b - a) // 16, src, a, "BE")
+
+    def cvt(k, part):
+        a, b = PT[part]
+        cp(X("L%d" % k, a // 16, b // 16), X(XB3[part], 0, (b - a) // 16))
+
+    def lst(k, a, b):
+        return X("L%d" % k, a // 16, b // 16)
+
+    def nbl(k, a=0, b=V):
+        return X("nbl", k * NW + a // 16, k * NW + b // 16)
+
+    def small_list(out, table):
+        act(X("tu"), G(X(table, 0, V), X("upl")), ACT.Identity)
+        wrap("psXC", 0, 4, "tu", 0, "BE")
+        return lambda: cp(out, X("psXC", 0, 4))
+
+    def twin(dst, src, j, on_g):
+        a, b = BK[j]
+        if j in on_g:
+            op("g", lambda: g.affine_select(T[dst][:, a:b], T[src][:, a:b], [[1, b - a]], ALU.is_ge, 0.0, 0, 0), [X(dst, a, b)], [X(src, a, b)])
+        else:
+            dma("s", X(dst, a, b), X(src, a, b))
+
+    def pair(j, l0, x0, l1, x1, start, stop):
+        a, b = BK[j]
+        mm(X(WB[j]), X(l0), X(x0, a, b), start, False)
+        mm(X(WB[j]), X(l1), X(x1, a, b), False, stop)
+
+    dma("s", X("pb"), dram(T.par))
+    if r > 0:
+        dma("a", X("upi"), dram(T.up))
+    dma("s", X("h"), dram(T.hf))
+    op("g", lambda: g.iota(T.ki[:, 0:1], [[0, 1]], 0, 1), [X("ki", 0, 1)], [])
+    op("g", lambda: g.iota(T.xi[:], [[1, 144]], 0, 0, allow_small_or_imprecise_dtypes=True), [X("xi")], [])
+    if r > 0:
+        send([("upi", "upr", None)], [r - 1])
+    op("g", lambda: g.iota(T.ck[:], [[NW, 5], [0, NW]], 0, 0, allow_small_or_imprecise_dtypes=True), [X("ck")], [])
+    op("g", lambda: g.iota(T.cc[:], [[0, 2], [1, NW]], 0, 0, allow_small_or_imprecise_dtypes=True), [X("cc")], [])
+    fill(X("C0", 0, V), 0.0)
+    ts(X("kj", 0, 1), X("ki", 0, 1), 15, None, ALU.bitwise_and)
+    ts(X("kj", 1, 2), X("ki", 0, 1), 112, None, ALU.bitwise_and)
+    cp(kf(0), X("ki", 0, 1))
+    cp(kf(1), X("kj", 0, 1))
+    ts(kf(2), X("kj", 1, 2), 15.0, None, ALU.add)
+    ts(X("I1"), X("xi", 0, 128), kf(0), None, ALU.is_equal)
+    ts(X("BD"), X("xi"), kf(2), 1024.0, ALU.is_equal, ALU.mult)
+    for name, w in (("I256", 256.0), ("Im1", -1.0), ("I2", 2.0), ("Im2", -2.0)):
+        act(X(name), X("I1"), ACT.Identity, scale=w)
+    ts(X("pa", 0, NW), X("pb"), 4032, None, ALU.bitwise_and)
+    ts(X("pa", NW, 2 * NW), X("pb"), 63, None, ALU.bitwise_and)
+    ts(kf(3), kf(1), 1.0, None, ALU.is_ge)
+    cp(X("hl"), X("pa"))
+    dma("s", X("C0", 0, V, rows=1), X("hl", 0, NW))
+    dma("a", X("C0", 0, V, rows=2), X("hl", NW, 2 * NW))
+    dma("s", X("b"), dram(T.bt))
+    dma("s", X("nbi"), dram(T.nb))
+    dma("s", X("d"), dram(T.dr))
+    ts(kf(5), kf(1), 0.0, None, ALU.is_equal)
+    ts(kf(4), kf(1), 2.0, kf(3), ALU.is_le, ALU.mult)
+    for name in ("P0", "gh", "PD"):
+        fill(X(name, 0, A), 1.0)
+    fill(X("absv", 0, 4), 2.0)
+    for name, w in (("BE", kf(4)), ("BF", kf(5))):
+        ts(X(name), X("xi"), kf(2), w, ALU.is_equal, ALU.mult)
+    if r == 0:
+        fill(X("ones"), 1.0)
+    if 0 < r < NR - 1:
+        fill(X("r0%d" % r), 0)
+        fill(X("r1%d" % r), 0)
+    for name, src, w in (("I512", "I1", 512.0), ("I768", "I1", 768.0), ("Ih", "I1", 0.5), ("I32", "I1", 1.0),
+                         ("BD2", "BD", 2.0), ("BDm", "BD", -1.0), ("BFm", "BF", -1.0)):
+        act(X(name), X(src), ACT.Identity, scale=w)
+    mklist(0, "C0")
+    mklist(1, "C0")
+    for j, (a, b) in enumerate(BK):
+        ts(X("P0", max(a, A), b), X("h", max(a, A), b), 0.5, None, ALU.mult)
+        if j < 2:
+            act(X("PD", max(a, A), b), X("h", max(a, A), b), ACT.Identity, scale=0.5)
+        else:
+            twin("PD", "P0", j, P_ON_G)
+    cvt(0, 0)
+
+    for e in range(2):
+        C = "C%d" % e
+        TT = [C, "T1", "T2", "T1", "T2", "T1"]
+        PP = ["P0" if e == 0 else "gh", "P1", "P0", "P1", "P0", "P1"]
+        SS = ["S0", "S1", "S0", "S1", "S0", "S1"]
+        mn, nn = "m%d%d" % (e, min(r, NR - 2)), "n%d%d" % (e, min(r, NR - 2))
+        rho = X("r%d%d" % (e, min(r, NR - 2)), 0, 4)
+
+        def bp(j):
+            act(X("U0", BK[j][0], BK[j][1]), X(WB[j]), ACT.Relu, bias=-256.0)
+            pair(j, "I2", "U0", "Im1", "b", True, False)
+
+        if e == 1:
+            tt(X("D0", 0, 1024), G(X("Z"), lst(0, 0, 1024)), X("gh", 0, 1024), ALU.mult)
+            cvt(0, 1)
+            tt(X("D0", 1024, V), G(X("Z"), lst(0, 1024, V)), X("gh", 1024, V), ALU.mult)
+            tt(X("D1", 0, V), G(X("U1"), lst(0, 0, V)), X("av"), ALU.mult)
+            for j in range(5):
+                pair(j, "I2", "U0", "Im1", "Z", True, False)
+                pair(j, "I1", "av", "Im2", "D0", False, False)
+
+        def jround(k, part):
+            a, b = PT[part]
+            act(X(TT[k + 1], a, b), G(X(TT[k], 0, V), lst(k, a, b)), ACT.Identity)
+
+        def pround(k, j):
+            a, b = BK[j]
+            tt(X(PP[k + 1], a, b), G(X(PP[k]), lst(k, a, b)), X("PD", a, b), ALU.mult)
+            if k < 4:
+                twin("PD", PP[k + 1], j, P_ON_G)
+
+        def extra(q):
+            if e == 0 and q in (2, 4, 5, 6, 7):
+                pair((2, 4, 5, 6, 7).index(q), "I1", "b", "I256", "h", True, True)
+            if e == 0 and q in (3, 5, 7):
+                bp((q - 3) // 2)
+            if e == 1 and 1 <= q < 6:
+                mm(X(WB[q - 1]), X("Im2"), X("D1", BK[q - 1][0], BK[q - 1][1]), False, False)
+
+        for k in range(4):
+            jround(k, 0)
+            pround(k, 0)
+            if k > 0 or e == 0:
+                cvt(k, 1)
+            mklist(0, TT[k + 1])
+            extra(2 * k)
+            jround(k, 1)
+            pround(k, 1)
+            pround(k, 2)
+            cvt(k + 1, 0)
+            mklist(1, TT[k + 1])
+            extra(2 * k + 1)
+            pround(k, 3)
+            pround(k, 4)
+            if e == 0 and k == 1 and r < NR - 1:
+                arrive("upr", r + 1, [r], None)
+                cp(X("upl"), X("upr"))
+        fin16 = small_list(X("l16"), TT[4]) if r < NR - 1 else None
+        if e == 0:
+            bp(3)
+            bp(4)
+        jround(4, 0)
+        fill(X("S0", 0, A), 0.0)
+        pround(4, 0)
+        cvt(4, 1)
+        mklist(0, TT[5])
+        for j, (a, b) in enumerate(BK):
+            if 0 < j < 4:
+                pround(4, j + 1)
+            if j == 1 and fin16:
+                fin16()
+            ts(X("s", a, b), X(PP[5], a, b), 0.0, 0.5, ALU.is_gt, ALU.subtract)
+            mm(X(WB[j]), X("I512" if e == 0 else "I768"), X("s", a, b), False, True)
+            lo = max(a, A)
+            act(X("S0", lo, b), X(WB[j], lo - a, 512), ACT.Abs)
+            twin("SD", "S0", j, S_ON_G)
+            if j == 0:
+                pround(4, 1)
+        if e == 0:
+            cp(X("nbl"), X("nbi"))
+        dma("s", X(C, 0, V, rows=0), X(PP[5], 0, V, rows=0))
+        cvt(5, 0)
+        if r < NR - 1:
+            ts(X("su" if e == 0 else mn), G(X("s"), X("upl")), 2.0, None, ALU.mult)
+        jround(4, 1)
+        mklist(1, TT[5])
+        fin32 = small_list(rho, TT[5]) if r < NR - 1 else None
+
+        def zround(k, between=()):
+            for j, (a, b) in enumerate(BK):
+                tt(X(SS[k + 1], a, b), G(X(SS[k]), lst(k, a, b)), X("SD", a, b), ALU.add)
+                if k < 4:
+                    twin("SD", SS[k + 1], j, S_ON_G[1:] if k == 1 else S_ON_G)
+                for f in between[j:j + 1] if j < 4 else between[4:]:
+                    f()
+
+        def cand(k):
+            act(X(C, (k + 1) * V, (k + 2) * V), G(X(C, 0, V), nbl(k)), ACT.Abs)
+
+        def pen_mm(k):
+            bank = XB3[k % 3]
+            mm(X(bank, 0, NW), X("I1"), X("absv"), True, False)
+            wrap(bank, 0, NW, C, (k + 1) * V, "BFm", start=False)
+
+        def pen_out(k):
+            act(X("pen", k * NW, k * NW + NW), X(XB3[k % 3], 0, NW), ACT.Relu, scale=2.0 ** 60)
+
+        def send_signs():
+            if e == 0:
+                tt(X(mn), G(X("h", 0, A), rho), X("su"), ALU.mult)
+            send([(mn, mn, 0)] + ([("r" + mn[1:], "r" + mn[1:], 1)] if r > 0 else []), later(r))
+
+        zround(0)
+        cvt(5, 1)
+        if r < NR - 1:
+            fin32()
+        cand(0)
+        wrap("psXC", 0, NW, C, 0, "BF")
+        act(X("absv", 4, NW), X("psXC", 4, NW), ACT.Abs)
+        pen_mm(0)
+        zround(1, [send_signs] if r < NR - 1 else [])
+        cand(1)
+        pen_out(0)
+        pen_mm(1)
+        zround(2)
+        for k in range(r):
+            arrive("m%d%d" % (e, k), k, later(k), part_of("m", k))
+            if k > 0:
+                arrive("r%d%d" % (e, k), k, later(k), part_of("r", k))
+        todo = []
+        if r == 0:
+            todo.append(lambda: cp(X("ah"), X("h", 0, A) if e == 0 else X("ones")))
+            if e == 0:
+                todo.append(lambda: cp(X("xb"), X("b", 0, A)))
+            todo.append(lambda: ts(X("xu"), X("ah"), -127.5, CB, ALU.mult, ALU.add))
+            todo.append(lambda: tt(X("kz"), X("xb"), X("ah"), ALU.mult))
+            todo.append(lambda: tt(X("kc"), X("kz"), X("xu"), ALU.add))
+        else:
+            cur = "m%d0" % e
+            for k in range(1, r):
+                nxt = "xs" if k == r - 1 else "x2"
+                todo.append(lambda k=k, nxt=nxt, cur=cur: tt(X(nxt), G(X(cur), X("r%d%d" % (e, k), 0, 4)), X("m%d%d" % (e, k)), ALU.mult))
+                cur = nxt
+            if e == 0:
+                todo.append(lambda cur=cur: tt(X("ah"), X(cur), X("h", 0, A), ALU.mult))
+            else:
+                todo.append(lambda cur=cur: cp(X("ah"), X(cur)))
+            todo.append(lambda cur=cur: tt(X("xb"), X(cur), X("b", 0, A) if e == 0 else X("xb"), ALU.mult))
+            todo.append(lambda: ts(X("xu"), X("ah"), -127.5, CB, ALU.mult, ALU.add))
+        cand(2)
+        pen_out(1)
+        pen_mm(2)
+        zround(3, todo)
+        if r < NR - 1:
+            cp(X("z1"), G(X(SS[4]), X("upl")))
+            tt(X("z2"), G(X(SS[4]), X("l16")), X("z1"), ALU.add)
+            tt(X("z1"), G(X("ah"), rho), X("z2"), ALU.mult)
+            tt(X(nn), G(X("xb"), rho), X("z1"), ALU.add)
+            send([(nn, nn, part_of("n", r))], later(r))
+        cand(3)
+        pen_out(2)
+        pen_mm(3)
+        zround(4)
+        for j, (a, b) in enumerate(BK):
+            mm(X(WB[j]), X("I32"), X("S1", a, b), True, False)
+        if e == 0:
+            act(X("ahr"), G(X("ah"), lst(5, 0, V)), ACT.Identity)
+        pen_out(3)
+        for k in range(r):
+            arrive("n%d%d" % (e, k), k, later(k), part_of("n", k))
+        if r > 0:
+            cur = "n%d0" % e
+            for k in range(1, r):
+                nxt = "z1" if k == 1 else "z2"
+                tt(X(nxt), G(X(cur), X("r%d%d" % (e, k), 0, 4)), X("n%d%d" % (e, k)), ALU.add)
+                cur = nxt
+            tt(X("ni"), X(cur), X("xb"), ALU.add)
+            ts(X("nj"), X("ni"), 255, None, ALU.bitwise_and)
+            tt(X("kz"), X("nj"), X("ah"), ALU.mult)
+            tt(X("kc"), X("kz"), X("xu"), ALU.add)
+        act(X("D0", 0, KS), G(X("kz"), lst(5, 0, KS)), ACT.Identity)
+        for j, (a, b) in enumerate(BK):
+            if b > KS:
+                cp(X("D0", max(a, KS), b), G(X("kz"), lst(5, max(a, KS), b)))
+            tt(X("tb", a, b), G(X("kc"), lst(5, a, b)), X("S1", a, b), ALU.add)
+            pair(j, "I1", "D0", "Im1", "tb", False, True)
+            act(X("Z", a, b), X(WB[j]), ACT.Abs, bias=CB)
+        if e == 1:
+            dma("s", dram(T.yx), X("Z"))
+
+        def key(k, src, base, a=0, b=V, stop=False):
+            wrap(KB[k][0], KB[k][1] + a // 16, (b - a) // 16, src, a, base, start=False, stop=stop)
+
+        def low(out, k):
+            tt(X(out), X(KB[k][0], KB[k][1], KB[k][1] + NW), X("best"), ALU.min)
+
+        def minus_z():
+            for j, (a, b) in enumerate(BK):
+                mm(X(WB[j]), X("Im1"), X("Z", a, b), True, False)
+
+        def apart(src):
+            for j, (a, b) in enumerate(BK):
+                mm(X(WB[j]), X("I1"), X(src, a, b), False, True)
+                act(X("U0", a, b), X(WB[j]), ACT.Abs)
+
+        minus_z()
+        for k in (2, 4, 0):
+            n = min(2 * NW, (5 - k) * NW)
+            mm(X(KB[k][0], 0, n), X("I1"), X("ck", k * NW, k * NW + n), True, False)
+            mm(X(KB[k][0], 0, n), X("I1"), X("cc", 0, n), False, False)
+        for k in range(1, 5):
+            mm(X(KB[k][0], KB[k][1], KB[k][1] + NW), X("I1"), X("pen", (k - 1) * NW, k * NW), False, False)
+        cp(X("Zp", ZS, V), G(X("Z"), lst(0, ZS, V)))
+        act(X("Zp", 0, ZS), G(X("Z"), lst(0, 0, ZS)), ACT.Identity)
+        tt(X("D0"), G(X("Zp"), nbl(0)), X("Z"), ALU.subtract)
+        apart("Zp")
+        minus_z()
+        key(0, "U0", "BD")
+        key(1, "D0", "BDm")
+        act(X("tb"), G(X("Zp"), nbl(2)), ACT.Identity)
+        tt(X("D1"), G(X("Zp"), nbl(1)), X("Z"), ALU.subtract)
+        ts(X("P0"), X("D0"), 0.0, None, ALU.max)
+        apart("tb")
+        key(1, "P0", "BD2", stop=True)
+        tt(X("D2", 0, RS), G(X("Zp"), nbl(3, 0, RS)), X("Z", 0, RS), ALU.subtract)
+        key(3, "U0", "BD")
+        act(X("U1", 0, H), X("D1", 0, H), ACT.Abs)
+        key(2, "U1", "BD", 0, H)
+        act(X("U1", H, V), X("D1", H, V), ACT.Abs)
+        tt(X("D2", RS, V), G(X("Zp"), nbl(3, RS, V)), X("Z", RS, V), ALU.subtract)
+        key(2, "U1", "BD", H, V, stop=True)
+        cp(X("best"), X("psXA", 0, NW))
+        ts(X("P1", RS, V), X("D2", RS, V), 0.0, None, ALU.max)
+        low("best", 1)
+        act(X("U0", 0, RS), X("D2", 0, RS), ACT.Abs)
+        key(4, "D2", "BDm", RS, V)
+        key(4, "P1", "BD2", RS, V)
+        key(4, "U0", "BD", 0, RS, stop=True)
+        if e == 0:
+            ts(X("gh", A, V), X("d", A, V), 128.0, 0.5, ALU.is_lt, ALU.subtract)
+            for j in range(5):
+                twin("PD", "gh", j, P_ON_G)
+            act(X("av"), X("d"), ACT.Abs, bias=-128.0)
+            for j in range(3):
+                pair(j, "I1", "s", "Ih", "ahr", True, True)
+        low("best", 2)
+        low("best", 3)
+        low("bi", 4)
+        ts(X("bj"), X("bi"), 1023, None, ALU.bitwise_and)
+        ts(X("idx"), X("bj"), 16.0, kf(1), ALU.mult, ALU.add)
+        if e == 0:
+            cp(X("C1", 0, 1024), G(X(C), X("idx", 0, 64)))
+            act(X("C1", 1024, V), G(X(C), X("idx", 64, NW)), ACT.Identity)
+            mklist(0, "C1")
+            cvt(0, 0)
+            for j in range(3, 5):
+                pair(j, "I1", "s", "Ih", "ahr", True, True)
+            mklist(1, "C1")
+            for j, (a, b) in enumerate(BK):
+                act(X("U1", a, b), X(WB[j]), ACT.Abs)
+                pair(j, "I1", "Z", "I512", "gh", True, True)
+            for j, (a, b) in enumerate(BK):
+                act(X("U0", a, b), X(WB[j]), ACT.Relu, bias=-256.0)
+        else:
+            for q in range(4):
+                a, b = 640 * q, 640 * q + 640
+                if q % 2 == 0:
+                    cp(X("T2", a, b), G(X(C), X("idx", a // 16, b // 16)))
+                else:
+                    act(X("T2", a, b), G(X(C), X("idx", a // 16, b // 16)), ACT.Identity)
+            for i in range(16):
+                mm(X("psXA", 0, NW), X("BE", 15 - i, 143 - i), X("T2", NW * i, NW * i + NW), i == 0, i == 15)
+            cp(X("po"), X("psXA", 0, NW))
+            dma("s", dram(T.yp), X("po"))
+
+    Q = {"v": g.vector, "a": g.scalar, "t": g.tensor, "g": g, "s": g.sync}
+    CS = {"v": "cv", "a": "ca", "t": "ct", "g": "cg"}
+    need = set()
+    for o in ops:
+        last = {}
+        for j in o["deps"]:
+            if ops[j]["sem"] is None:
+                last[ops[j]["q"]] = max(last.get(ops[j]["q"], -1), j)
+        need.update(last.values())
+    cnt, mark = {q: 0 for q in CS}, {}
+    for j, o in enumerate(ops):
+        if o["sem"] is None:
+            if j in need:
+                cnt[o["q"]] += 1
+                mark[j] = (CS[o["q"]], cnt[o["q"]])
+        elif o["sem"]:
+            mark[j] = (o["sem"], o["n"])
+    seen, waited = {q: {} for q in Q}, set()
+    for j, o in enumerate(ops):
+        if o["q"] == "x":
+            continue
+        want = {}
+        for d in o["deps"]:
+            if d in mark:
+                want[mark[d][0]] = max(want.get(mark[d][0], 0), mark[d][1])
+        for s, n in want.items():
+            if seen[o["q"]].get(s, 0) < n:
+                Q[o["q"]].wait_ge(T.sem[s], n)
+                seen[o["q"]][s] = n
+                waited.add(s)
+        ins = o["fn"]()
+        if j in mark:
+            ins.then_inc(T.sem[mark[j][0]], 1 if o["sem"] is None else o["n"])
+    for j, o in enumerate(ops):
+        if o["sem"] and o["sem"] not in waited:
+            g.sync.wait_ge(T.sem[o["sem"]], o["n"])
+    if sent[0]:
+        g.wait_ge(T.sem.sent, sent[0])

@@ -2,71 +2,89 @@ from concourse.bass import DstId, RemoteDMATransfer
 from concourse.mybir import AluOpType as ALU, ActivationFunctionType as ACT
 
 V, A, NW = 2560, 64, 160
-CB = 34816.0
-P_ON_G, S_ON_G = (0, 2), (0, 2, 4)
-ZS, RS, KS = 1280, 1280, 1792
+W, C0 = V + 16, A // 16
+XS, XN = A + 2048, 28
+CB = 33280.0
+P_ON_G, S_ON_G = (0, 2, 4), (0, 2, 4)
+NB, TAIL = 5, 128
+ZS, KS, CS0 = (1280, 1280), (2560, 2048), 512
+VOTES = [[[("v", V)], [("s", V)], [("v", V)], [("s", 1024), ("b", V)]],
+         [[("v", V)], [("s", V)], [("v", V)], [("s", 512), ("b", V)]]]
+LATE = {(0, 4): (0, 1), (1, 1): (1, 0), (1, 4): (1, 1), (2, 1): (2, 0), (2, 4): (2, 1)}
+AHEAD = {0: (3, 0), 1: (3, 1), 2: (3, 1)}
+HS = 2048
+OUT = [(0, 800), (800, 1600), (1600, 2080), (2080, V)]
+PIECE = 900
+CY, GAM, WAKE, LOOK, ROUNDS = 0.00083, 1.45, 0.1, 0.05, 2
 
 SCRATCH = {}
-for _n in ("h", "b", "d", "gh", "av", "P0", "P1", "PD", "T1", "T2", "s", "ahr", "Z", "Zp", "tb", "D0", "D1", "D2", "U0", "U1"):
+for _n in ("b", "d", "PD", "GD", "s", "Hh", "Z", "Zp", "tb", "D0", "D1", "D2", "D3", "U0", "U1", "U2", "U3", "U4"):
     SCRATCH[_n] = ("sbuf", [128, V], "bfloat16")
+for _n in ("h", "gs", "P0", "P1", "T1", "T2"):
+    SCRATCH[_n] = ("sbuf", [128, W], "bfloat16")
 for _n in ("C0", "C1"):
     SCRATCH[_n] = ("sbuf", [128, 5 * V], "bfloat16")
 for _n in ("S0", "S1", "SD"):
-    SCRATCH[_n] = ("sbuf", [128, V], "float32")
+    SCRATCH[_n] = ("sbuf", [128, W], "float32")
 for _n in range(6):
     SCRATCH["L%d" % _n] = ("sbuf", [128, NW], "uint16")
 for _n in ("W0", "W1", "W2", "W3", "W4", "XA", "XB", "XC"):
     SCRATCH["ps" + _n] = ("psum", [128, 512], "float32")
-for _n in ("I1", "Im1", "I2", "Im2", "I256", "I512", "I768", "Ih"):
+for _n in ("I1", "Im1", "I2", "I256", "I512", "I1024", "IV"):
     SCRATCH[_n] = ("sbuf", [128, 128], "bfloat16")
-for _n in ("BE", "BD", "BD2", "BDm", "BF", "BFm"):
+for _n in ("BE", "BG"):
     SCRATCH[_n] = ("sbuf", [128, 144], "bfloat16")
+for _n in ("G8", "G16", "Gm8", "GF", "GFm"):
+    SCRATCH[_n] = ("sbuf", [128, 8], "bfloat16")
 SCRATCH.update({
-    "I32": ("sbuf", [128, 128], "float32"), "xi": ("sbuf", [128, 144], "float32"),
-    "ck": ("sbuf", [128, 5 * NW], "bfloat16"), "cc": ("sbuf", [128, 2 * NW], "bfloat16"),
-    "ki": ("sbuf", [128, 4], "int32"), "kj": ("sbuf", [128, 4], "int32"), "kf": ("sbuf", [128, 8], "float32"),
-    "pb": ("sbuf", [128, NW], "int32"), "pa": ("sbuf", [128, 2 * NW], "int32"), "hl": ("sbuf", [128, 2 * NW], "bfloat16"),
+    "I32": ("sbuf", [128, 128], "float32"), "xi": ("sbuf", [128, 144], "float32"), "xg": ("sbuf", [128, 8], "float32"),
+    "ck": ("sbuf", [128, 5 * 256], "bfloat16"), "cc": ("sbuf", [128, NW], "bfloat16"),
+    "ki": ("sbuf", [128, 4], "int32"), "kj": ("sbuf", [128, 4], "int32"), "kf": ("sbuf", [128, 12], "float32"),
+    "pb": ("sbuf", [128, NW], "int32"), "hl": ("sbuf", [128, 2 * NW], "bfloat16"),
+    "dq": ("sbuf", [128, NW], "bfloat16"), "dw": ("sbuf", [128, NW], "bfloat16"),
     "nbi": ("sbuf", [128, 4 * NW], "int32"), "nbl": ("sbuf", [128, 4 * NW], "uint16"),
-    "upi": ("sbuf", [128, 4], "int32"), "upr": ("sbuf", [128, 4], "int32"), "upl": ("sbuf", [128, 4], "uint16"),
-    "l16": ("sbuf", [128, 4], "uint16"), "tu": ("sbuf", [128, A], "bfloat16"),
-    "absv": ("sbuf", [128, NW], "bfloat16"), "pen": ("sbuf", [128, 4 * NW], "bfloat16"),
-    "best": ("sbuf", [128, NW], "float32"), "bi": ("sbuf", [128, NW], "int32"), "bj": ("sbuf", [128, NW], "int32"),
-    "idx": ("sbuf", [128, NW], "uint16"), "po": ("sbuf", [128, NW], "float32"),
+    "upi": ("sbuf", [128, 4], "int32"), "upr": ("sbuf", [128, 4], "int32"), "l8": ("sbuf", [128, 32], "uint16"),
+    "tu": ("sbuf", [128, 8 * A], "bfloat16"), "z8": ("sbuf", [128, 8 * A], "float32"), "rl": ("sbuf", [128, 16], "uint16"),
+    "an": ("sbuf", [128, NW], "bfloat16"), "av": ("sbuf", [128, 256], "bfloat16"), "pen": ("sbuf", [128, 4 * 256], "bfloat16"),
+    "best": ("sbuf", [128, 256], "float32"), "bi": ("sbuf", [128, 256], "int32"), "bj": ("sbuf", [128, 256], "int32"),
+    "kb": ("sbuf", [128, 256], "bfloat16"), "idx": ("sbuf", [128, NW], "uint16"), "po": ("sbuf", [128, NW], "float32"),
     "ni": ("sbuf", [128, A], "int32"), "nj": ("sbuf", [128, A], "int32"),
-    "ah": ("sbuf", [128, A], "bfloat16"), "kz": ("sbuf", [128, A], "bfloat16"),
 })
-for _n in ("su", "x2", "xs", "xb", "xu", "z1", "z2", "kc", "ones"):
+for _n in ("ha", "sen", "ids", "id1", "id2", "kz"):
+    SCRATCH[_n] = ("sbuf", [128, A], "bfloat16")
+for _n in ("xb", "xu", "kc"):
     SCRATCH[_n] = ("sbuf", [128, A], "float32")
+MW = 2 * A + 8
 for _e in range(2):
     for _r in range(3):
-        SCRATCH["m%d%d" % (_e, _r)] = ("sbuf", [128, A], "bfloat16")
-        SCRATCH["n%d%d" % (_e, _r)] = ("sbuf", [128, A], "float32")
-        SCRATCH["r%d%d" % (_e, _r)] = ("sbuf", [128, A], "uint16")
+        SCRATCH["m%d%d" % (_e, _r)] = ("sbuf", [128, MW], "float32")
+for _r in range(3):
+    SCRATCH["u%d" % _r] = ("sbuf", [128, 2 * A], "float32")
 
 SEMAPHORES = ["cv", "ca", "ct", "cg", "sent", "upr"] + ["d%d" % _n for _n in range(90)] + \
-    ["%s%d%d" % (_k, _e, _r) for _k in "mnr" for _e in range(2) for _r in range(3)]
+    ["m%d%d" % (_e, _r) for _e in range(2) for _r in range(3)]
 
 
-def rank_program(g, core, T, topo):
-    r = T.rank_of(core)
-    if r is None:
-        return
+def calls(g, T, topo, r):
     NR = len(T.cores)
     ops, acc, ndma, sent = [], {}, [0], [0]
 
-    def X(name, a=0, b=None, step=1, rows=None):
+    def X(name, a=0, b=None, step=1, rows=None, top=128):
         t = T[name]
         b = t.shape[1] if b is None else b
         if rows is not None:
             ap = t[rows:128:16, a:b]
         else:
-            ap = t[:, a:b] if step == 1 else t[:, a:b:step]
-        return (ap, [(name, a, b, rows)])
+            ap = t[0:top, a:b] if step == 1 else t[0:top, a:b:step]
+        return (ap, [(name, a, b, rows)], (b - a + step - 1) // step)
 
     def G(win, off):
-        return (win[0].indirect(off[0]), win[1] + off[1])
+        return (win[0].indirect(off[0]), win[1] + off[1], 16 * off[2])
 
-    def op(q, fn, outs, ins, sem=None, n=1):
+    def size(x):
+        return 2 if SCRATCH[x[1][0][0]][2] in ("bfloat16", "uint16") else 4
+
+    def op(q, fn, outs, ins, cost, lat=0.0, sem=None, n=1, wire=0.0, lands=(), adds=False):
         me, deps = len(ops), set()
         for wr, regs in ((False, ins), (True, outs)):
             for x in regs:
@@ -75,52 +93,79 @@ def rank_program(g, core, T, topo):
                 for name, a, b, rows in x[1]:
                     w = wr
                     if name.startswith("ps"):
-                        a, b, w = 0, 512, True
+                        a, b, w = 0, 512, not adds
                     keep = []
                     for (a2, b2, rows2, w2, j) in acc.get(name, []):
                         hit = a < b2 and a2 < b and (rows is None or rows2 is None or rows == rows2)
-                        if hit and (w or w2) and j != me and not (q == "t" and ops[j]["q"] == "t"):
+                        if hit and (w or w2) and j != me:
                             deps.add(j)
                         if not (w and rows is None and a <= a2 and b2 <= b):
                             keep.append((a2, b2, rows2, w2, j))
                     acc[name] = keep + [(a, b, rows, w, me)]
-        ops.append({"q": q, "fn": fn, "deps": deps, "sem": sem, "n": n})
+        ops.append({"q": q, "fn": fn, "deps": deps, "sem": sem, "n": n, "cost": cost, "lat": lat, "after": set(), "wire": wire, "lands": lands})
+        return me
+
+    def cyc(o, a, per):
+        return 0.06 + CY * max(64, o[2] * (GAM if len(a[1]) > 1 else per))
 
     def dma(q, out, in_):
         k = ndma[0]
         ndma[0] += 1
         e = g.sync if q == "s" else g.scalar
-        op(q, lambda: e.dma_start(out[0], in_[0]), [out], [in_], sem="d%d" % k, n=16)
+        side = out if out[1] else in_
+        nbytes = side[2] * size(side) * (128 if side[1][0][3] is None else 8)
+        return op(q, lambda: e.dma_start(out[0], in_[0]), [out], [in_], 0.06, 1.3, sem="d%d" % k, n=16, wire=nbytes / 250e3)
 
-    def dram(t):
-        return (t[:], [])
+    def dram(ap):
+        return (ap, [], 0)
 
     def tt(o, a, b, alu):
-        op("v", lambda: g.vector.tensor_tensor(o[0], a[0], b[0], alu), [o], [a, b])
+        return op("v", lambda: g.vector.tensor_tensor(o[0], a[0], b[0], alu), [o], [a, b], cyc(o, a, 1 if a[1][0][0].startswith("ps") else 2))
 
     def ts(o, a, s1, s2, o0, o1=None):
         v1 = s1[0] if isinstance(s1, tuple) else s1
         v2 = s2[0] if isinstance(s2, tuple) else s2
+        c = cyc(o, a, 0.5 if size(o) + size(a) == 4 else 1)
         if o1 is None:
-            op("v", lambda: g.vector.tensor_scalar(o[0], a[0], v1, None, o0), [o], [a, s1])
-        else:
-            op("v", lambda: g.vector.tensor_scalar(o[0], a[0], v1, v2, o0, o1), [o], [a, s1, s2])
+            return op("v", lambda: g.vector.tensor_scalar(o[0], a[0], v1, None, o0), [o], [a, s1], c)
+        return op("v", lambda: g.vector.tensor_scalar(o[0], a[0], v1, v2, o0, o1), [o], [a, s1, s2], c)
 
     def cp(o, a):
-        op("v", lambda: g.vector.tensor_copy(o[0], a[0]), [o], [a])
+        return op("v", lambda: g.vector.tensor_copy(o[0], a[0]), [o], [a], cyc(o, a, 0.5 if size(o) + size(a) == 4 else 1))
 
     def fill(o, c):
-        op("v", lambda: g.vector.memset(o[0], c), [o], [])
+        return op("v", lambda: g.vector.memset(o[0], c), [o], [], cyc(o, o, size(o) / 4))
 
-    def act(o, a, f, bias=0.0, scale=1.0):
-        op("a", lambda: g.scalar.activation(o[0], a[0], f, bias=bias, scale=scale), [o], [a])
+    def act(o, a, f=ACT.Identity, bias=0.0, scale=1.0):
+        sv = scale[0] if isinstance(scale, tuple) else scale
+        return op("a", lambda: g.scalar.activation(o[0], a[0], f, bias=bias, scale=sv), [o], [a, scale], 0.02 + cyc(o, a, 1))
 
-    def mm(o, l, x, start, stop):
-        op("t", lambda: g.tensor.matmul(o[0], l[0], x[0], start, stop), [o], [l, x])
+    def gcp(o, a):
+        return op("g", lambda: g.affine_select(o[0], a[0], [[1, o[2]]], ALU.is_ge, 0.0, 0, 0), [o], [a], 0.17 + 2 * CY * o[2])
+
+    def iota(name, pattern, step=0, b=None):
+        o = X(name, 0, b)
+        if SCRATCH[name][2] == "int32":
+            return op("g", lambda: g.iota(o[0], pattern, 0, step), [o], [], 0.13 + 2 * CY * o[2])
+        return op("g", lambda: g.iota(o[0], pattern, 0, step, allow_small_or_imprecise_dtypes=True), [o], [], 0.13 + 2 * CY * o[2])
+
+    def mms(items, start, stop):
+        def fn():
+            for n, (o, l, x) in enumerate(items):
+                ins = g.tensor.matmul(o[0], l[0], x[0], start and n == 0, stop and n == len(items) - 1)
+            return ins
+        return op("t", fn, [o for o, l, x in items], [y for o, l, x in items for y in (l, x)],
+                  sum(0.01 + CY / 2 * max(min(64, l[2]), x[2]) * size(x) ** 2 / 4 for o, l, x in items), adds=not (start or stop))
 
     def wrap(bank, c0, n, src, col, base, start=True, stop=True):
-        for i in range(16):
-            mm(X(bank, c0, c0 + n), X(base, 15 - i, 143 - i), X(src, col + i, col + 16 * n, 16), start and i == 0, stop and i == 15)
+        for q in range(0, 16, 4):
+            mms([(X(bank, c0, c0 + n), X(base, 15 - i, 143 - i), X(src, col + i, col + 16 * n, 16)) for i in range(q, q + 4)], start and q == 0, stop and q == 12)
+
+    def turn(bank, c0, part, src, col, sel, stop):
+        a, b = XP[part]
+        c0 += 128 * part
+        for q in range(0, 16, 8):
+            mms([(X(bank, c0 + i, c0 + 128, 16, top=(b - a) // 16), X(src, col + a + i, col + b, 16), X(sel)) for i in range(q, q + 8)], False, stop and q == 8)
 
     def later(k):
         return list(range(k + 1, NR))
@@ -129,405 +174,436 @@ def rank_program(g, core, T, topo):
         es = [e for e in topo.engines(T.cores[k], T.cores[dsts[0]]) if all(e in topo.engines(T.cores[k], T.cores[x]) for x in dsts)]
         return es if part is None else es[part * len(es) // 2:(part + 1) * len(es) // 2]
 
-    def part_of(kind, k):
-        if kind == "r":
-            return 1
-        return 0 if kind == "m" or k == 0 else None
+    def part_of(k):
+        return 0 if k == 0 else None
 
-    def send(items, dsts):
+    def send(src, land, part, dsts, lat):
         ids = [DstId(rid=topo.addr(T.cores[k])[0], pnc=topo.addr(T.cores[k])[1]) for k in dsts]
-        tr = []
-        for src, land, part in items:
-            es = engines(r, dsts, part)
-            sent[0] += len(es)
-            tr.append(RemoteDMATransfer(dst_ids=ids, dma_engine_mask=sum(1 << e for e in es), remote_sem=T.sem[land],
-                                        srcs=[T[src][:]], dsts=[T[land][:] for _ in dsts]))
-        op("g", lambda: g.remote_dma_fused(tr, local_sem=T.sem.sent), [], [X(x[0]) for x in items], sem="")
+        es = engines(r, dsts, part)
+        sent[0] += len(es)
+        tr = RemoteDMATransfer(dst_ids=ids, dma_engine_mask=sum(1 << e for e in es), remote_sem=T.sem[land],
+                               srcs=[src[0]], dsts=[X(land, 0, src[2])[0] for _ in dsts])
+        return op("g", lambda: g.remote_dma_fused([tr], local_sem=T.sem.sent), [], [src], 0.8 if sent[0] > len(es) else 3.0, lat, sem="",
+                  lands=[(k, land) for k in dsts])
 
     def arrive(name, frm, dsts, part):
-        op("x", None, [X(name)], [], sem=name, n=len(engines(frm, dsts, part)))
+        return op("x", None, [X(name)], [], 0.0, sem=name, n=len(engines(frm, dsts, part)))
 
-    H = V // 2
     BK = [(512 * j, 512 * j + 512) for j in range(5)]
+    BN = [(max(a, A), b) for a, b in BK]
     WB = ["psW%d" % j for j in range(5)]
     XB3 = ["psXA", "psXB", "psXC"]
-    PT = [(0, 1024), (1024, V)]
-    KB = {0: ("psXA", 0), 1: ("psXA", NW), 2: ("psXB", 0), 3: ("psXB", NW), 4: ("psXC", 0)}
+    PT = [(A, 1024), (1024, V)]
+    XP = [(A, XS), (XS, V)]
+    KB = {0: ("psXA", 0), 1: ("psXA", 256), 2: ("psXB", 0), 3: ("psXB", 256), 4: ("psXC", 0)}
+    sends = r < NR - 1
 
     def kf(j):
         return X("kf", j, j + 1)
 
-    def mklist(part, src):
+    def mklist(k, part, src):
         a, b = PT[part]
         wrap(XB3[part], 0, (b - a) // 16, src, a, "BE")
-
-    def cvt(k, part):
-        a, b = PT[part]
-        cp(X("L%d" % k, a // 16, b // 16), X(XB3[part], 0, (b - a) // 16))
+        cp(lst(k, a, b), X(XB3[part], 0, (b - a) // 16))
 
     def lst(k, a, b):
         return X("L%d" % k, a // 16, b // 16)
 
-    def nbl(k, a=0, b=V):
+    def nbl(k, a=A, b=V):
         return X("nbl", k * NW + a // 16, k * NW + b // 16)
 
-    def small_list(out, table):
-        act(X("tu"), G(X(table, 0, V), X("upl")), ACT.Identity)
-        wrap("psXC", 0, 4, "tu", 0, "BE")
-        return lambda: cp(out, X("psXC", 0, 4))
-
-    def twin(dst, src, j, on_g):
-        a, b = BK[j]
-        if j in on_g:
-            op("g", lambda: g.affine_select(T[dst][:, a:b], T[src][:, a:b], [[1, b - a]], ALU.is_ge, 0.0, 0, 0), [X(dst, a, b)], [X(src, a, b)])
+    def twin(dst, src, a, b, on_g):
+        if on_g:
+            gcp(X(dst, a, b), X(src, a, b))
         else:
             dma("s", X(dst, a, b), X(src, a, b))
 
-    def pair(j, l0, x0, l1, x1, start, stop):
-        a, b = BK[j]
-        mm(X(WB[j]), X(l0), X(x0, a, b), start, False)
-        mm(X(WB[j]), X(l1), X(x1, a, b), False, stop)
+    def wb(j, a, b):
+        return X(WB[j], a - BK[j][0], b - BK[j][0]) if j < 5 else X("psXC", 0, b - a)
 
-    dma("s", X("pb"), dram(T.par))
+    def terms(j, items, start, stop, a, b):
+        return mms([(wb(j, a, b), X(l), X(x, a, b)) for l, x in items], start, stop)
+
+    def pieces(a, b, most=PIECE):
+        n = -((a - b) // most)
+        cut = [a + (b - a) * i // n // 32 * 32 for i in range(n)] + [b]
+        return list(zip(cut, cut[1:]))
+
+    def halves(a, b):
+        return pieces(a, b, 1400)
+
+    def way_at(ways, a):
+        return [way for way, b in ways if a < b][0]
+
+    RB = pieces(A, V, (V - A) // NB + 32)
+    LB = BN
+
+    dma("s", X("pb"), dram(T.par[:]))
+    counts = [iota("ki", [[0, 1]], 1, 1), iota("xi", [[1, 144]]), iota("xg", [[16, 8]]), iota("cc", [[16, NW]])]
     if r > 0:
-        dma("a", X("upi"), dram(T.up))
-    dma("s", X("h"), dram(T.hf))
-    op("g", lambda: g.iota(T.ki[:, 0:1], [[0, 1]], 0, 1), [X("ki", 0, 1)], [])
-    op("g", lambda: g.iota(T.xi[:], [[1, 144]], 0, 0, allow_small_or_imprecise_dtypes=True), [X("xi")], [])
-    if r > 0:
-        send([("upi", "upr", None)], [r - 1])
-    op("g", lambda: g.iota(T.ck[:], [[NW, 5], [0, NW]], 0, 0, allow_small_or_imprecise_dtypes=True), [X("ck")], [])
-    op("g", lambda: g.iota(T.cc[:], [[0, 2], [1, NW]], 0, 0, allow_small_or_imprecise_dtypes=True), [X("cc")], [])
-    fill(X("C0", 0, V), 0.0)
+        dma("a", X("upi"), dram(T.up[:]))
+        counts.append(send(X("upi"), "upr", None, [r - 1], 8.0))
+        ops[counts[-1]]["after"].update(counts[:-1])
+    dma("a", X("ha"), dram(T.hf[:, 0:A]))
+    dma("s", X("h", A, HS), dram(T.hf[:, A:HS]))
+    ops[iota("ck", [[1, 5], [0, 256]])]["after"].update(counts)
+    fill(X("C0", A, V), 0.0)
     ts(X("kj", 0, 1), X("ki", 0, 1), 15, None, ALU.bitwise_and)
     ts(X("kj", 1, 2), X("ki", 0, 1), 112, None, ALU.bitwise_and)
     cp(kf(0), X("ki", 0, 1))
-    cp(kf(1), X("kj", 0, 1))
-    ts(kf(2), X("kj", 1, 2), 15.0, None, ALU.add)
-    ts(X("I1"), X("xi", 0, 128), kf(0), None, ALU.is_equal)
-    ts(X("BD"), X("xi"), kf(2), 1024.0, ALU.is_equal, ALU.mult)
-    for name, w in (("I256", 256.0), ("Im1", -1.0), ("I2", 2.0), ("Im2", -2.0)):
-        act(X(name), X("I1"), ACT.Identity, scale=w)
-    ts(X("pa", 0, NW), X("pb"), 4032, None, ALU.bitwise_and)
-    ts(X("pa", NW, 2 * NW), X("pb"), 63, None, ALU.bitwise_and)
-    ts(kf(3), kf(1), 1.0, None, ALU.is_ge)
-    cp(X("hl"), X("pa"))
-    dma("s", X("C0", 0, V, rows=1), X("hl", 0, NW))
-    dma("a", X("C0", 0, V, rows=2), X("hl", NW, 2 * NW))
-    dma("s", X("b"), dram(T.bt))
-    dma("s", X("nbi"), dram(T.nb))
-    dma("s", X("d"), dram(T.dr))
+    cp(X("kf", 1, 3), X("kj", 0, 2))
+    ts(kf(10), kf(2), 15.0, None, ALU.add)
     ts(kf(5), kf(1), 0.0, None, ALU.is_equal)
-    ts(kf(4), kf(1), 2.0, kf(3), ALU.is_le, ALU.mult)
-    for name in ("P0", "gh", "PD"):
-        fill(X(name, 0, A), 1.0)
-    fill(X("absv", 0, 4), 2.0)
-    for name, w in (("BE", kf(4)), ("BF", kf(5))):
-        ts(X(name), X("xi"), kf(2), w, ALU.is_equal, ALU.mult)
+    ts(kf(6), kf(1), 1.0, None, ALU.is_equal)
+    ts(kf(7), kf(1), 2.0, None, ALU.is_equal)
+    ts(kf(4), kf(6), kf(7), None, ALU.add)
+    ts(kf(8), kf(5), -0.75, 1.0, ALU.mult, ALU.add)
+    ts(kf(9), kf(5), 1.0, None, ALU.add)
+    ts(X("hl", 0, NW), X("pb"), 8.0, 0.0, ALU.subtract, ALU.max)
+    tt(X("hl", NW, 2 * NW), X("pb"), X("hl", 0, NW), ALU.subtract)
+    first = [dma("s", X("C0", 0, V, rows=1), X("hl", 0, NW)), dma("s", X("C0", 0, V, rows=2), X("hl", NW, 2 * NW))]
+    first.append(dma("s", X("h", HS, V), dram(T.hf[:, HS:V])))
+    ops[first[2]]["deps"].update(ops[first[1]]["deps"])
+    ops[first[2]]["after"].update(ops[first[1]]["deps"])
+    late = {}
+    for k, name, src in ((0, "b", T.bt), (1, "d", T.dr), (2, "nbi", T.nb)):
+        n = T[name].shape[1] // 2
+        late[k] = [dma("s", X(name, a, a + n), dram(src[:, a:a + n])) for a in (0, n)]
+        ops[late[k][0]]["after"].update(first)
+    ops[dma("s", X("dq"), dram(T.dr[0:128:16, :]))]["after"].update(late[1])
+    ts(X("I1"), X("xi", 0, 128), kf(0), None, ALU.is_equal)
+    for name, w in (("BE", kf(4)), ("BG", kf(6))):
+        ts(X(name), X("xi"), kf(10), w, ALU.is_equal, ALU.mult)
+    ts(X("G8"), X("xg"), kf(2), 8.0, ALU.is_equal, ALU.mult)
+    ts(X("GF"), X("xg"), kf(2), kf(5), ALU.is_equal, ALU.mult)
+    for name, src, w in (("I256", "I1", 256.0), ("I2", "I1", 2.0), ("Im1", "I1", -1.0), ("I512", "I1", 512.0), ("I1024", "I1", 1024.0),
+                         ("I32", "I1", 1.0), ("IV", "I1", float(V)), ("G16", "G8", 2.0), ("Gm8", "G8", -1.0), ("GFm", "GF", -1.0)):
+        act(X(name), X(src), scale=w)
+    ts(X("id1"), X("xi", 0, A), kf(6), 1.0, ALU.mult, ALU.add)
+    ts(X("id2"), X("xi", 0, A), kf(6), kf(9), ALU.mult, ALU.add)
+    act(X("ids"), X("xi", 0, A), scale=kf(7))
+    ts(X("sen"), X("xi", 0, A), -1.0, kf(6), ALU.is_gt, ALU.mult)
+    for name in ("C0", "C1", "T1", "T2"):
+        act(X(name, 0, A), X("sen"), scale=float(V))
+    for name in ("T1", "T2"):
+        act(X(name, V, W), X("sen", 0, 16), scale=float(V))
+    tt(X("h", 0, A), X("id2"), X("ha"), ALU.mult)
+    tt(X("P1", 0, A), X("id1"), X("ha"), ALU.mult)
+    gcp(X("P0", 0, A), X("P1", 0, A))
+    for name in ("P1", "P0"):
+        act(X(name, V, W), X("xi", 0, 16), bias=1.0, scale=0.0)
+    for name in ("S0", "S1"):
+        gcp(X(name, 0, A), X("b", 0, A))
+        act(X(name, V, W), X("xi", 0, 16), scale=0.0)
+    for name in ("L0", "idx"):
+        ts(X(name, 0, C0), X("cc", 0, C0), kf(1), None, ALU.add)
     if r == 0:
-        fill(X("ones"), 1.0)
-    if 0 < r < NR - 1:
-        fill(X("r0%d" % r), 0)
-        fill(X("r1%d" % r), 0)
-    for name, src, w in (("I512", "I1", 512.0), ("I768", "I1", 768.0), ("Ih", "I1", 0.5), ("I32", "I1", 1.0),
-                         ("BD2", "BD", 2.0), ("BDm", "BD", -1.0), ("BFm", "BF", -1.0)):
-        act(X(name), X(src), ACT.Identity, scale=w)
-    mklist(0, "C0")
-    mklist(1, "C0")
-    for j, (a, b) in enumerate(BK):
-        ts(X("P0", max(a, A), b), X("h", max(a, A), b), 0.5, None, ALU.mult)
-        if j < 2:
-            act(X("PD", max(a, A), b), X("h", max(a, A), b), ACT.Identity, scale=0.5)
-        else:
-            twin("PD", "P0", j, P_ON_G)
-    cvt(0, 0)
+        fill(X("u0", 0, A), 1.0)
+        fill(X("kz"), 0.0)
+        fill(X("kc"), CB - 127.5)
+    for part, (a, b) in enumerate([(A, HS), (HS, V)]):
+        mklist(0, part, "C0")
+        ts(X("PD", a, b), X("h", a, b), kf(8), None, ALU.mult)
+    cp(X("nbl"), X("nbi"))
+    if sends:
+        arrive("upr", r + 1, [r], None)
+        cp(X("l8", 0, 4), X("upr"))
+    for a, b in pieces(A, V):
+        act(X("gs", a, b), X("d", a, b), ACT.Sign, bias=127.5, scale=-1.0)
+    act(X("dw"), X("dq"), ACT.Sign, bias=127.5, scale=-1.0)
+    act(X("dq"), X("dw"), scale=0.25)
+    gcp(X("gs", 0, A), X("id2"))
 
     for e in range(2):
         C = "C%d" % e
-        TT = [C, "T1", "T2", "T1", "T2", "T1"]
-        PP = ["P0" if e == 0 else "gh", "P1", "P0", "P1", "P0", "P1"]
+        TT = [C, "T1", "T2", "T1", "T2"]
+        PP = ["h" if e == 0 else "gs", "P1", "P0", "P1", "P0", "P1"]
         SS = ["S0", "S1", "S0", "S1", "S0", "S1"]
-        mn, nn = "m%d%d" % (e, min(r, NR - 2)), "n%d%d" % (e, min(r, NR - 2))
-        rho = X("r%d%d" % (e, min(r, NR - 2)), 0, 4)
+        mn = "m%d%d" % (e, r)
+        uh = X("u0" if r == 0 else "m%d0" % e if r == 1 else "u%d" % (r - 1), 0, A)
 
-        def bp(j):
-            act(X("U0", BK[j][0], BK[j][1]), X(WB[j]), ACT.Relu, bias=-256.0)
-            pair(j, "I2", "U0", "Im1", "b", True, False)
-
+        jump = {}
+        for k in range(5):
+            for j, (a, b) in enumerate(RB if k < 4 else LB):
+                n = tt(X(PP[k + 1], a, b), G(X(PP[k], 0, V if k == 0 else W), lst(k, a, b)), X("GD" if k == 0 and e == 1 else "PD", a, b), ALU.mult)
+                if e == 0 and (k, j) in LATE:
+                    ops[late[LATE[k, j][0]][LATE[k, j][1]]]["deps"].add(n)
+                if k < 4:
+                    twin("PD", PP[k + 1], a, b, j in P_ON_G)
+            for part, (a, b) in enumerate(PT if k < 4 else []):
+                jump[k, part] = act(X(TT[k + 1], a, b), G(X(TT[k], 0, V if k == 0 else W), lst(k, a, b)))
+                mklist(k + 1, part, TT[k + 1])
+            if sends and 1 <= k < 4:
+                n = 2 << k
+                act(X("tu", 16 * n, 32 * n), G(X(TT[k + 1]), X("l8", 0, n)))
+                wrap("psXC", 0, n, "tu", 16 * n, "BE")
+                cp(X("l8", n, 2 * n), X("psXC", 0, n))
+        gcp(X(C, 0, A), X("ids"))
         if e == 1:
-            tt(X("D0", 0, 1024), G(X("Z"), lst(0, 0, 1024)), X("gh", 0, 1024), ALU.mult)
-            cvt(0, 1)
-            tt(X("D0", 1024, V), G(X("Z"), lst(0, 1024, V)), X("gh", 1024, V), ALU.mult)
-            tt(X("D1", 0, V), G(X("U1"), lst(0, 0, V)), X("av"), ALU.mult)
-            for j in range(5):
-                pair(j, "I2", "U0", "Im1", "Z", True, False)
-                pair(j, "I1", "av", "Im2", "D0", False, False)
-
-        def jround(k, part):
-            a, b = PT[part]
-            act(X(TT[k + 1], a, b), G(X(TT[k], 0, V), lst(k, a, b)), ACT.Identity)
-
-        def pround(k, j):
-            a, b = BK[j]
-            tt(X(PP[k + 1], a, b), G(X(PP[k]), lst(k, a, b)), X("PD", a, b), ALU.mult)
-            if k < 4:
-                twin("PD", PP[k + 1], j, P_ON_G)
-
-        def extra(q):
-            if e == 0 and q in (2, 4, 5, 6, 7):
-                pair((2, 4, 5, 6, 7).index(q), "I1", "b", "I256", "h", True, True)
-            if e == 0 and q in (3, 5, 7):
-                bp((q - 3) // 2)
-            if e == 1 and 1 <= q < 6:
-                mm(X(WB[q - 1]), X("Im2"), X("D1", BK[q - 1][0], BK[q - 1][1]), False, False)
+            for a, b in PT:
+                tt(X("D1", a, b), G(X("Hh"), lst(0, a, b)), X("d", a, b), ALU.mult)
+            for a, b in BN:
+                act(X("Zp", a, b), G(X("Z"), lst(0, a, b)))
+        for j, (a, b) in enumerate(LB):
+            if e == 0:
+                terms(j, [("I1", "b"), ("I256", "h")], True, True, a, b)
+                act(X("U0", a, b), wb(j, a, b), ACT.Relu, bias=-256.0)
+                terms(j, [("I2", "U0"), ("Im1", "b")], True, False, a, b)
+            else:
+                terms(j, [("I1", "Z"), ("I512", "gs")], True, False, a, b)
+                terms(j, [("I2", "D1")], False, False, a, b)
+                terms(j, [("Im1", "Zp")], False, True, a, b)
+                n = act(X("SD", a, b), wb(j, a, b), ACT.Abs)
+                if j in AHEAD:
+                    ops[jump[AHEAD[j]]]["after"].add(n)
+                terms(j, [("I32", "SD")], True, False, a, b)
+            ts(X("s", a if j else 0, b), X(PP[5], a if j else 0, b), 0.0, 0.5, ALU.is_gt, ALU.subtract)
+            terms(j, [("I512" if e == 0 else "I1024", "s")], False, True, a, b)
+            act(X("S0", a, b), wb(j, a, b), ACT.Abs, bias=0.0 if e == 0 else -512.0)
+        for j, (a, b) in enumerate(RB):
+            twin("SD", "S0", a, b, j in S_ON_G)
+        dma("a", X(C, 0, V, rows=0), X(PP[5], 0, V, rows=0))
+        if sends:
+            act(X("tu", 0, A), G(X(PP[5], 0, V), X("l8", 0, 4)))
+            act(X(mn, 0, A), X("tu", 0, A), ACT.Sign)
+            if r > 0:
+                wrap("psXC", 0, 4, "tu", 0, "BG")
+                act(X(mn, 2 * A, 2 * A + 4), X("psXC", 0, 4), ACT.Abs)
+                act(X(mn, 2 * A + 4, MW), X("psXC", 0, 4), ACT.Abs)
+        wrap("psXA", 0, NW, PP[5], 0, "BG")
+        act(X("an"), X("psXA", 0, NW), ACT.Abs)
+        ts(X("L5"), X("an"), 1.0, None, ALU.subtract)
+        mms([(X("psXB", 0, 256), X("I1"), X("ck", 0, 256))], True, False)
+        for part in (1, 0):
+            turn("psXB", 0, part, PP[5], 0, "GF", part == 0)
+        act(X("av"), X("psXB", 0, 256), ACT.Abs)
 
         for k in range(4):
-            jround(k, 0)
-            pround(k, 0)
-            if k > 0 or e == 0:
-                cvt(k, 1)
-            mklist(0, TT[k + 1])
-            extra(2 * k)
-            jround(k, 1)
-            pround(k, 1)
-            pround(k, 2)
-            cvt(k + 1, 0)
-            mklist(1, TT[k + 1])
-            extra(2 * k + 1)
-            pround(k, 3)
-            pround(k, 4)
-            if e == 0 and k == 1 and r < NR - 1:
-                arrive("upr", r + 1, [r], None)
-                cp(X("upl"), X("upr"))
-        fin16 = small_list(X("l16"), TT[4]) if r < NR - 1 else None
-        if e == 0:
-            bp(3)
-            bp(4)
-        jround(4, 0)
-        fill(X("S0", 0, A), 0.0)
-        pround(4, 0)
-        cvt(4, 1)
-        mklist(0, TT[5])
-        for j, (a, b) in enumerate(BK):
-            if 0 < j < 4:
-                pround(4, j + 1)
-            if j == 1 and fin16:
-                fin16()
-            ts(X("s", a, b), X(PP[5], a, b), 0.0, 0.5, ALU.is_gt, ALU.subtract)
-            mm(X(WB[j]), X("I512" if e == 0 else "I768"), X("s", a, b), False, True)
-            lo = max(a, A)
-            act(X("S0", lo, b), X(WB[j], lo - a, 512), ACT.Abs)
-            twin("SD", "S0", j, S_ON_G)
-            if j == 0:
-                pround(4, 1)
-        if e == 0:
-            cp(X("nbl"), X("nbi"))
-        dma("s", X(C, 0, V, rows=0), X(PP[5], 0, V, rows=0))
-        cvt(5, 0)
-        if r < NR - 1:
-            ts(X("su" if e == 0 else mn), G(X("s"), X("upl")), 2.0, None, ALU.mult)
-        jround(4, 1)
-        mklist(1, TT[5])
-        fin32 = small_list(rho, TT[5]) if r < NR - 1 else None
+            bank = XB3[(k + 2) % 3]
+            mms([(X(bank, 0, 256), X("I1"), X("av"))], True, False)
+            for a, b in pieces(A, V):
+                act(X(C, (k + 1) * V + a, (k + 1) * V + b), G(X(C, 0, V), nbl(k, a, b)), ACT.Abs)
+            for part in (1, 0):
+                turn(bank, 0, part, C, (k + 1) * V, "GFm", part == 0)
+            act(X("pen", k * 256, k * 256 + 256), X(bank, 0, 256), ACT.Relu, scale=2.0 ** 60)
 
-        def zround(k, between=()):
-            for j, (a, b) in enumerate(BK):
+        for k in range(5):
+            for j, (a, b) in enumerate(RB if k < 4 else BN):
                 tt(X(SS[k + 1], a, b), G(X(SS[k]), lst(k, a, b)), X("SD", a, b), ALU.add)
                 if k < 4:
-                    twin("SD", SS[k + 1], j, S_ON_G[1:] if k == 1 else S_ON_G)
-                for f in between[j:j + 1] if j < 4 else between[4:]:
-                    f()
-
-        def cand(k):
-            act(X(C, (k + 1) * V, (k + 2) * V), G(X(C, 0, V), nbl(k)), ACT.Abs)
-
-        def pen_mm(k):
-            bank = XB3[k % 3]
-            mm(X(bank, 0, NW), X("I1"), X("absv"), True, False)
-            wrap(bank, 0, NW, C, (k + 1) * V, "BFm", start=False)
-
-        def pen_out(k):
-            act(X("pen", k * NW, k * NW + NW), X(XB3[k % 3], 0, NW), ACT.Relu, scale=2.0 ** 60)
-
-        def send_signs():
-            if e == 0:
-                tt(X(mn), G(X("h", 0, A), rho), X("su"), ALU.mult)
-            send([(mn, mn, 0)] + ([("r" + mn[1:], "r" + mn[1:], 1)] if r > 0 else []), later(r))
-
-        zround(0)
-        cvt(5, 1)
-        if r < NR - 1:
-            fin32()
-        cand(0)
-        wrap("psXC", 0, NW, C, 0, "BF")
-        act(X("absv", 4, NW), X("psXC", 4, NW), ACT.Abs)
-        pen_mm(0)
-        zround(1, [send_signs] if r < NR - 1 else [])
-        cand(1)
-        pen_out(0)
-        pen_mm(1)
-        zround(2)
-        for k in range(r):
-            arrive("m%d%d" % (e, k), k, later(k), part_of("m", k))
-            if k > 0:
-                arrive("r%d%d" % (e, k), k, later(k), part_of("r", k))
-        todo = []
-        if r == 0:
-            todo.append(lambda: cp(X("ah"), X("h", 0, A) if e == 0 else X("ones")))
-            if e == 0:
-                todo.append(lambda: cp(X("xb"), X("b", 0, A)))
-            todo.append(lambda: ts(X("xu"), X("ah"), -127.5, CB, ALU.mult, ALU.add))
-            todo.append(lambda: tt(X("kz"), X("xb"), X("ah"), ALU.mult))
-            todo.append(lambda: tt(X("kc"), X("kz"), X("xu"), ALU.add))
-        else:
-            cur = "m%d0" % e
-            for k in range(1, r):
-                nxt = "xs" if k == r - 1 else "x2"
-                todo.append(lambda k=k, nxt=nxt, cur=cur: tt(X(nxt), G(X(cur), X("r%d%d" % (e, k), 0, 4)), X("m%d%d" % (e, k)), ALU.mult))
-                cur = nxt
-            if e == 0:
-                todo.append(lambda cur=cur: tt(X("ah"), X(cur), X("h", 0, A), ALU.mult))
-            else:
-                todo.append(lambda cur=cur: cp(X("ah"), X(cur)))
-            todo.append(lambda cur=cur: tt(X("xb"), X(cur), X("b", 0, A) if e == 0 else X("xb"), ALU.mult))
-            todo.append(lambda: ts(X("xu"), X("ah"), -127.5, CB, ALU.mult, ALU.add))
-        cand(2)
-        pen_out(1)
-        pen_mm(2)
-        zround(3, todo)
-        if r < NR - 1:
-            cp(X("z1"), G(X(SS[4]), X("upl")))
-            tt(X("z2"), G(X(SS[4]), X("l16")), X("z1"), ALU.add)
-            tt(X("z1"), G(X("ah"), rho), X("z2"), ALU.mult)
-            tt(X(nn), G(X("xb"), rho), X("z1"), ALU.add)
-            send([(nn, nn, part_of("n", r))], later(r))
-        cand(3)
-        pen_out(2)
-        pen_mm(3)
-        zround(4)
-        for j, (a, b) in enumerate(BK):
-            mm(X(WB[j]), X("I32"), X("S1", a, b), True, False)
-        if e == 0:
-            act(X("ahr"), G(X("ah"), lst(5, 0, V)), ACT.Identity)
-        pen_out(3)
-        for k in range(r):
-            arrive("n%d%d" % (e, k), k, later(k), part_of("n", k))
+                    twin("SD", SS[k + 1], a, b, j in S_ON_G)
+            if k == 1 and sends:
+                act(X("z8"), G(X(SS[2]), X("l8")))
+                mms([(X("psW0", 0, A), X("I32"), X("z8", A * q, A * q + A)) for q in range(8)], True, True)
+                act(X(mn, A, 2 * A), X("psW0", 0, A))
+                send(X(mn, 0, MW if r > 0 else 2 * A), mn, part_of(r), later(r), 3.0)
         if r > 0:
-            cur = "n%d0" % e
+            for k in range(r):
+                arrive("m%d%d" % (e, k), k, later(k), part_of(k))
+            cur = "m%d0" % e
+            if r == 1:
+                cp(X("ni"), X(cur, A, 2 * A))
             for k in range(1, r):
-                nxt = "z1" if k == 1 else "z2"
-                tt(X(nxt), G(X(cur), X("r%d%d" % (e, k), 0, 4)), X("n%d%d" % (e, k)), ALU.add)
+                msg, nxt = "m%d%d" % (e, k), "u%d" % k
+                ts(X("rl", 8 * k - 8, 8 * k), X(msg, 2 * A, MW), 1.0, None, ALU.subtract)
+                tt(X(nxt), G(X(cur, 0, A), X("rl", 8 * k - 8, 8 * k)), X(msg, 0, 2 * A), ALU.mult)
+                tt(X(nxt, A, 2 * A) if k < r - 1 else X("ni"), G(X(cur, A, 2 * A), X("rl", 8 * k - 8, 8 * k - 4)), X(nxt, A, 2 * A), ALU.add)
                 cur = nxt
-            tt(X("ni"), X(cur), X("xb"), ALU.add)
+            act(X("xu"), uh, bias=CB, scale=-127.5)
             ts(X("nj"), X("ni"), 255, None, ALU.bitwise_and)
-            tt(X("kz"), X("nj"), X("ah"), ALU.mult)
+            tt(X("kz"), X("nj"), uh, ALU.mult)
             tt(X("kc"), X("kz"), X("xu"), ALU.add)
-        act(X("D0", 0, KS), G(X("kz"), lst(5, 0, KS)), ACT.Identity)
-        for j, (a, b) in enumerate(BK):
-            if b > KS:
-                cp(X("D0", max(a, KS), b), G(X("kz"), lst(5, max(a, KS), b)))
+        for a, b in BK:
+            (act if a < KS[e] else cp)(X("D0", a, b), G(X("kz"), lst(5, a, b)))
+        for j, (a, b) in enumerate(LB):
+            a = a if j else 0
+            terms(j, [("I32", "S1")], True, False, a, b)
+            terms(j, [("I1", "D0")], False, False, a, b)
             tt(X("tb", a, b), G(X("kc"), lst(5, a, b)), X("S1", a, b), ALU.add)
-            pair(j, "I1", "D0", "Im1", "tb", False, True)
-            act(X("Z", a, b), X(WB[j]), ACT.Abs, bias=CB)
+            terms(j, [("Im1", "tb")], False, True, a, b)
+            placed = act(X("Z", a, b), wb(j, a, b), ACT.Abs, bias=CB)
         if e == 1:
-            dma("s", dram(T.yx), X("Z"))
-
-        def key(k, src, base, a=0, b=V, stop=False):
-            wrap(KB[k][0], KB[k][1] + a // 16, (b - a) // 16, src, a, base, start=False, stop=stop)
-
-        def low(out, k):
-            tt(X(out), X(KB[k][0], KB[k][1], KB[k][1] + NW), X("best"), ALU.min)
-
-        def minus_z():
-            for j, (a, b) in enumerate(BK):
-                mm(X(WB[j]), X("Im1"), X("Z", a, b), True, False)
-
-        def apart(src):
-            for j, (a, b) in enumerate(BK):
-                mm(X(WB[j]), X("I1"), X(src, a, b), False, True)
-                act(X("U0", a, b), X(WB[j]), ACT.Abs)
-
-        minus_z()
-        for k in (2, 4, 0):
-            n = min(2 * NW, (5 - k) * NW)
-            mm(X(KB[k][0], 0, n), X("I1"), X("ck", k * NW, k * NW + n), True, False)
-            mm(X(KB[k][0], 0, n), X("I1"), X("cc", 0, n), False, False)
-        for k in range(1, 5):
-            mm(X(KB[k][0], KB[k][1], KB[k][1] + NW), X("I1"), X("pen", (k - 1) * NW, k * NW), False, False)
-        cp(X("Zp", ZS, V), G(X("Z"), lst(0, ZS, V)))
-        act(X("Zp", 0, ZS), G(X("Z"), lst(0, 0, ZS)), ACT.Identity)
-        tt(X("D0"), G(X("Zp"), nbl(0)), X("Z"), ALU.subtract)
-        apart("Zp")
-        minus_z()
-        key(0, "U0", "BD")
-        key(1, "D0", "BDm")
-        act(X("tb"), G(X("Zp"), nbl(2)), ACT.Identity)
-        tt(X("D1"), G(X("Zp"), nbl(1)), X("Z"), ALU.subtract)
-        ts(X("P0"), X("D0"), 0.0, None, ALU.max)
-        apart("tb")
-        key(1, "P0", "BD2", stop=True)
-        tt(X("D2", 0, RS), G(X("Zp"), nbl(3, 0, RS)), X("Z", 0, RS), ALU.subtract)
-        key(3, "U0", "BD")
-        act(X("U1", 0, H), X("D1", 0, H), ACT.Abs)
-        key(2, "U1", "BD", 0, H)
-        act(X("U1", H, V), X("D1", H, V), ACT.Abs)
-        tt(X("D2", RS, V), G(X("Zp"), nbl(3, RS, V)), X("Z", RS, V), ALU.subtract)
-        key(2, "U1", "BD", H, V, stop=True)
-        cp(X("best"), X("psXA", 0, NW))
-        ts(X("P1", RS, V), X("D2", RS, V), 0.0, None, ALU.max)
-        low("best", 1)
-        act(X("U0", 0, RS), X("D2", 0, RS), ACT.Abs)
-        key(4, "D2", "BDm", RS, V)
-        key(4, "P1", "BD2", RS, V)
-        key(4, "U0", "BD", 0, RS, stop=True)
-        if e == 0:
-            ts(X("gh", A, V), X("d", A, V), 128.0, 0.5, ALU.is_lt, ALU.subtract)
-            for j in range(5):
-                twin("PD", "gh", j, P_ON_G)
-            act(X("av"), X("d"), ACT.Abs, bias=-128.0)
-            for j in range(3):
-                pair(j, "I1", "s", "Ih", "ahr", True, True)
-        low("best", 2)
-        low("best", 3)
-        low("bi", 4)
-        ts(X("bj"), X("bi"), 1023, None, ALU.bitwise_and)
-        ts(X("idx"), X("bj"), 16.0, kf(1), ALU.mult, ALU.add)
-        if e == 0:
-            cp(X("C1", 0, 1024), G(X(C), X("idx", 0, 64)))
-            act(X("C1", 1024, V), G(X(C), X("idx", 64, NW)), ACT.Identity)
-            mklist(0, "C1")
-            cvt(0, 0)
-            for j in range(3, 5):
-                pair(j, "I1", "s", "Ih", "ahr", True, True)
-            mklist(1, "C1")
-            for j, (a, b) in enumerate(BK):
-                act(X("U1", a, b), X(WB[j]), ACT.Abs)
-                pair(j, "I1", "Z", "I512", "gh", True, True)
-            for j, (a, b) in enumerate(BK):
-                act(X("U0", a, b), X(WB[j]), ACT.Relu, bias=-256.0)
+            dma("s", dram(T.yx[:]), X("Z"))
         else:
-            for q in range(4):
-                a, b = 640 * q, 640 * q + 640
-                if q % 2 == 0:
-                    cp(X("T2", a, b), G(X(C), X("idx", a // 16, b // 16)))
-                else:
-                    act(X("T2", a, b), G(X(C), X("idx", a // 16, b // 16)), ACT.Identity)
-            for i in range(16):
-                mm(X("psXA", 0, NW), X("BE", 15 - i, 143 - i), X("T2", NW * i, NW * i + NW), i == 0, i == 15)
-            cp(X("po"), X("psXA", 0, NW))
-            dma("s", dram(T.yp), X("po"))
+            ops[dma("s", X("GD", A, V), X("gs", A, V))]["deps"].add(placed)
+            dma("s", X("GD", 0, V, rows=0), X("dq"))
+            tt(X("xb"), uh, X("b", 0, A), ALU.mult)
+            for name in ("P0", "P1"):
+                gcp(X(name, 0, A), X("id1"))
+            for name in ("S0", "S1"):
+                gcp(X(name, 0, A), X("xb"))
+            for a, b in BK:
+                tt(X("Hh", a, b), G(uh, lst(5, a, b)), X("s", a, b), ALU.mult)
 
+        for k in (0, 2, 4):
+            n = min(512, (5 - k) * 256)
+            mms([(X(KB[k][0], 0, n), X("I1"), X("ck", k * 256, k * 256 + n))], True, False)
+        left = {bank: 0 for bank in XB3}
+        plan = list(enumerate([[("s", V)]] + VOTES[e]))
+        for k, ways in plan:
+            left[KB[k][0]] += 2 + sum(1 for a, b in XP if way_at(ways, a) == "v")
+
+        def key(k, src, sel, part):
+            left[KB[k][0]] -= 1
+            turn(KB[k][0], KB[k][1], part, src, 0, sel, False)
+            if left[KB[k][0]] == 0:
+                mms([(X(KB[q][0], KB[q][1], KB[q][1] + 256), X("I1"), X("pen", (q - 1) * 256, q * 256))
+                     for q in range(1, 5) if KB[q][0] == KB[k][0]], False, True)
+
+        for a, b in halves(ZS[e], V) if ZS[e] < V else []:
+            cp(X("Zp", a, b), G(X("Z"), lst(0, a, b)))
+        for a, b in halves(0, ZS[e]):
+            act(X("Zp", a, b), G(X("Z"), lst(0, a, b)))
+        for k, ways in plan:
+            D, U, a0, todo = "D%d" % (k - 1), "U%d" % k, A, [0, 1]
+            for way, b0 in ways:
+                cuts = [(a0, XS), (XS, b0)] if a0 < XS < b0 else [(a0, b0)]
+                for a, b in [x for c in cuts for x in halves(*c)]:
+                    if way != "s":
+                        tt(X(D, a, b), G(X("Zp"), nbl(k - 1, a, b)), X("Z", a, b), ALU.subtract)
+                    elif k > 0:
+                        act(X(D, a, b), G(X("Zp"), nbl(k - 1, a, b)))
+                    if way == "b":
+                        act(X(U, a, b), X(D, a, b), ACT.Abs)
+                for a, b in cuts if way == "v" else []:
+                    key(k, D, "Gm8", XP.index((a, b)))
+                    ts(X(U, a, b), X(D, a, b), 0.0, None, ALU.max)
+                for j in range(5) if way == "s" else []:
+                    a, b = max(a0, BK[j][0]), min(b0, BK[j][1])
+                    if a < b:
+                        terms(j, [("Im1", "Z")], True, False, a, b)
+                        terms(j, [("I1", D if k > 0 else "Zp")], False, True, a, b)
+                        act(X(U, a, b), wb(j, a, b), ACT.Abs)
+                while todo and XP[todo[0]][1] <= b0:
+                    part = todo.pop(0)
+                    key(k, U, "G16" if way_at(ways, XP[part][0]) == "v" else "G8", part)
+                a0 = b0
+        act(X("best"), X("psXA", 0, 256))
+        mms([(X("psW4", C0, NW), X("I1"), X("cc", C0, NW))], True, False)
+        for k in range(1, 5):
+            tt(X("best" if k < 4 else "bi"), X(KB[k][0], KB[k][1], KB[k][1] + 256), X("best"), ALU.min)
+        ts(X("bj"), X("bi"), 7, None, ALU.bitwise_and)
+        cp(X("kb"), X("bj"))
+        mms([(X("psW4", C0, C0 + 128), X("kb", 0, 128), X("IV")),
+             (X("psW4", C0 + 128, NW), X("kb", 128, 256, top=XN), X("IV", 0, XN, top=XN))], False, True)
+        ts(X("idx", C0, NW), X("psW4", C0, NW), kf(1), None, ALU.add)
+        if e == 0:
+            cp(X("C1", A, CS0), G(X(C), X("idx", A // 16, CS0 // 16)))
+            for part, (a, b) in enumerate(PT):
+                act(X("C1", max(a, CS0), b), G(X(C), X("idx", max(a, CS0) // 16, b // 16)))
+                mklist(0, part, "C1")
+        else:
+            for q, (a, b) in enumerate(OUT):
+                (cp if q % 2 == 0 else act)(X("T2", a, b), G(X(C), X("idx", a // 16, b // 16)))
+                mms([(X("psXA", 0, NW), X("BE", 15 - i, 143 - i), X("T2", NW * i, NW * i + NW)) for i in range(a // NW, b // NW)], q == 0, b == V)
+            cp(X("po"), X("psXA", 0, NW))
+            dma("s", dram(T.yp[:]), X("po"))
+    return ops, sent[0]
+
+
+def arrange(ops, pre, succ, weight, back):
+    free, done, count, order = {}, {}, [len(p) for p in pre], []
+    ready = {j: ops[j]["lat"] * back for j, p in enumerate(pre) if not p}
+    while ready:
+        start = {j: max(t, free.get(ops[j]["Q"], 0.0)) for j, t in ready.items()}
+        j0 = min(start, key=lambda j: (start[j], -weight[j]))
+        j = max((x for x in start if ops[x]["Q"] == ops[j0]["Q"] and start[x] <= start[j0] + LOOK), key=lambda x: weight[x])
+        o = ops[j]
+        free[o["Q"]] = done[j] = start[j] + o["cost"]
+        if o["wire"]:
+            free[o["Q"][0]] = done[j] = max(free.get(o["Q"][0], 0.0), done[j]) + o["wire"]
+        done[j] += o["lat"] * (1 - back)
+        order.append(j)
+        del ready[j]
+        for s in succ[j]:
+            count[s] -= 1
+            if count[s] == 0:
+                ready[s] = ops[s]["lat"] * back + max(done[d] + (0.0 if ops[d]["q"] == ops[s]["q"] == "t" else WAKE) for d in pre[s])
+    return order, done
+
+
+def place(ops, pre, succ, weight, back):
+    busy, start, done, count = {}, {}, {}, [len(p) for p in pre]
+    ready = {j for j, p in enumerate(pre) if not p}
+
+    def fit(q, t, c):
+        line = busy.setdefault(q, [])
+        for n, (a, b) in enumerate(line + [(1e9, 1e9)]):
+            if t + c <= a + 1e-9:
+                break
+            t = max(t, b)
+        line.insert(n, (t, t + c))
+        return t
+
+    while ready:
+        j = max(ready, key=lambda x: (weight[x], -x))
+        ready.remove(j)
+        o = ops[j]
+        t = o["lat"] * back + max([done[d] + (0.0 if ops[d]["q"] == o["q"] == "t" else WAKE) for d in pre[j]], default=0.0)
+        if o["wire"] and back:
+            t = fit(o["Q"][0], t, o["wire"]) + o["wire"]
+        start[j] = fit(o["Q"], t, o["cost"])
+        done[j] = start[j] + o["cost"]
+        if o["wire"] and not back:
+            done[j] = fit(o["Q"][0], done[j], o["wire"]) + o["wire"]
+        done[j] += o["lat"] * (1 - back)
+        for s in succ[j]:
+            count[s] -= 1
+            if count[s] == 0:
+                ready.add(s)
+    return sorted(start, key=lambda x: (start[x], done[x])), done
+
+
+ORDER, RULES = {}, [arrange, arrange, place, place, place]
+
+
+def orders(g, T, topo):
+    if not ORDER:
+        ops, pre, home = [], [], []
+        for k in range(len(T.cores)):
+            base = len(ops)
+            for j, o in enumerate(calls(g, T, topo, k)[0]):
+                ops.append(dict(o, Q=(k, o["q"])))
+                pre.append({base + d for d in o["deps"] | o["after"]})
+                home.append((k, j))
+        landing = {(o["Q"][0], o["sem"]): j for j, o in enumerate(ops) if o["q"] == "x"}
+        for j, o in enumerate(ops):
+            for x in o["lands"]:
+                pre[landing[x]].add(j)
+        succ = [set() for _ in pre]
+        for j, p in enumerate(pre):
+            for d in p:
+                succ[d].add(j)
+        order, head = arrange(ops, pre, succ, [-j for k, j in home], 0)
+        for rule in RULES:
+            order, tail = rule(ops, succ, pre, head, 1)
+            order, head = rule(ops, pre, succ, tail, 0)
+        ORDER["end"] = max(head.values())
+        for j in order:
+            ORDER.setdefault(home[j][0], []).append(home[j][1])
+    return ORDER
+
+
+def rank_program(g, core, T, topo):
+    r = T.rank_of(core)
+    if r is None:
+        return
+    order = orders(g, T, topo)[r]
+    ops, sent = calls(g, T, topo, r)
     Q = {"v": g.vector, "a": g.scalar, "t": g.tensor, "g": g, "s": g.sync}
     CS = {"v": "cv", "a": "ca", "t": "ct", "g": "cg"}
+    place = {j: n for n, j in enumerate(order)}
     need = set()
     for o in ops:
+        o["deps"] = {d for d in o["deps"] if not (o["q"] == "t" and ops[d]["q"] == "t")}
         last = {}
-        for j in o["deps"]:
-            if ops[j]["sem"] is None:
-                last[ops[j]["q"]] = max(last.get(ops[j]["q"], -1), j)
+        for d in o["deps"]:
+            if ops[d]["sem"] is None:
+                last[ops[d]["q"]] = max(last.get(ops[d]["q"], d), d, key=lambda x: place[x])
         need.update(last.values())
     cnt, mark = {q: 0 for q in CS}, {}
-    for j, o in enumerate(ops):
+    for j in order:
+        o = ops[j]
         if o["sem"] is None:
             if j in need:
                 cnt[o["q"]] += 1
@@ -535,7 +611,8 @@ def rank_program(g, core, T, topo):
         elif o["sem"]:
             mark[j] = (o["sem"], o["n"])
     seen, waited = {q: {} for q in Q}, set()
-    for j, o in enumerate(ops):
+    for j in order:
+        o = ops[j]
         if o["q"] == "x":
             continue
         want = {}
@@ -550,8 +627,8 @@ def rank_program(g, core, T, topo):
         ins = o["fn"]()
         if j in mark:
             ins.then_inc(T.sem[mark[j][0]], 1 if o["sem"] is None else o["n"])
-    for j, o in enumerate(ops):
+    for o in ops:
         if o["sem"] and o["sem"] not in waited:
             g.sync.wait_ge(T.sem[o["sem"]], o["n"])
-    if sent[0]:
-        g.wait_ge(T.sem.sent, sent[0])
+    if sent:
+        g.wait_ge(T.sem.sent, sent)

@@ -3,19 +3,19 @@ from concourse.mybir import AluOpType as ALU, ActivationFunctionType as ACT
 
 V, A, NW = 2560, 64, 160
 W, C0 = V + 16, A // 16
-XS, XN = A + 2048, 28
+XS = 13 * NW
+XW = XS // 16
 CB = 33280.0
-P_ON_G, S_ON_G = (0, 2, 4), (0, 2, 4)
-NB, TAIL = 5, 128
-ZS, KS, CS0 = (1280, 1280), (2560, 2048), 512
-VOTES = [[[("v", V)], [("s", V)], [("v", V)], [("s", 1024), ("b", V)]],
-         [[("v", V)], [("s", V)], [("v", V)], [("s", 512), ("b", V)]]]
-LATE = {(0, 4): (0, 1), (1, 1): (1, 0), (1, 4): (1, 1), (2, 1): (2, 0), (2, 4): (2, 1)}
-AHEAD = {0: (3, 0), 1: (3, 1), 2: (3, 1)}
-HS = 2048
-OUT = [(0, 800), (800, 1600), (1600, 2080), (2080, V)]
-PIECE = 900
-CY, GAM, WAKE, LOOK, ROUNDS = 0.00083, 1.45, 0.1, 0.05, 2
+ON_G = (0, 2, 4)
+ZS, HS = 1280, 2048
+VOTES = [[("s", 320), ("b", V)], [("s", V)], [("v", V)], [("v", V)]]
+LATE = {(0, 4): ("b", 1), (1, 1): ("d", 0), (1, 4): ("d", 1), (2, 1): ("nbi", 0), (2, 4): ("nbi", 1)}
+PT = [(A, 1056), (1056, V)]
+NEW = [(A, 1056), (1056, XS), (XS, V)]
+XP = [(A, XS), (XS, V)]
+EV = [(A, 1024), (1024, 1536), (1536, 2048), (2048, V)]
+OUT = [(0, 1120, "a")] + [(_n, _n + NW, "v") for _n in range(1120, XS, NW)]
+CY, GAM, WAKE, LOOK = 0.00083, 1.45, 0.17, 0.05
 
 SCRATCH = {}
 for _n in ("b", "d", "PD", "GD", "s", "Hh", "Z", "Zp", "tb", "D0", "D1", "D2", "D3", "U0", "U1", "U2", "U3", "U4"):
@@ -28,17 +28,18 @@ for _n in ("S0", "S1", "SD"):
     SCRATCH[_n] = ("sbuf", [128, W], "float32")
 for _n in range(6):
     SCRATCH["L%d" % _n] = ("sbuf", [128, NW], "uint16")
-for _n in ("W0", "W1", "W2", "W3", "W4", "XA", "XB", "XC"):
+SCRATCH["psW"] = ("psum", [128, V], "float32")
+for _n in ("XA", "XB", "XC"):
     SCRATCH["ps" + _n] = ("psum", [128, 512], "float32")
-for _n in ("I1", "Im1", "I2", "I256", "I512", "I1024", "IV"):
+for _n in ("I1", "Im1", "I2", "I256", "I512", "I1024"):
     SCRATCH[_n] = ("sbuf", [128, 128], "bfloat16")
-for _n in ("BE", "BG"):
+for _n in ("BD", "BE", "BG"):
     SCRATCH[_n] = ("sbuf", [128, 144], "bfloat16")
-for _n in ("G8", "G16", "Gm8", "GF", "GFm"):
+for _n in ("G1", "Gk", "G2k", "Gmk", "G8k", "GE", "GF", "GFm"):
     SCRATCH[_n] = ("sbuf", [128, 8], "bfloat16")
 SCRATCH.update({
     "I32": ("sbuf", [128, 128], "float32"), "xi": ("sbuf", [128, 144], "float32"), "xg": ("sbuf", [128, 8], "float32"),
-    "ck": ("sbuf", [128, 5 * 256], "bfloat16"), "cc": ("sbuf", [128, NW], "bfloat16"),
+    "ck": ("sbuf", [128, 5 * 128], "bfloat16"), "cc": ("sbuf", [128, NW], "bfloat16"),
     "ki": ("sbuf", [128, 4], "int32"), "kj": ("sbuf", [128, 4], "int32"), "kf": ("sbuf", [128, 12], "float32"),
     "pb": ("sbuf", [128, NW], "int32"), "hl": ("sbuf", [128, 2 * NW], "bfloat16"),
     "dq": ("sbuf", [128, NW], "bfloat16"), "dw": ("sbuf", [128, NW], "bfloat16"),
@@ -48,9 +49,10 @@ SCRATCH.update({
     "an": ("sbuf", [128, NW], "bfloat16"), "av": ("sbuf", [128, 256], "bfloat16"), "pen": ("sbuf", [128, 4 * 256], "bfloat16"),
     "best": ("sbuf", [128, 256], "float32"), "bi": ("sbuf", [128, 256], "int32"), "bj": ("sbuf", [128, 256], "int32"),
     "kb": ("sbuf", [128, 256], "bfloat16"), "idx": ("sbuf", [128, NW], "uint16"), "po": ("sbuf", [128, NW], "float32"),
+    "low": ("sbuf", [128, 512], "bfloat16"), "tie": ("sbuf", [128, 512], "bfloat16"), "pf": ("sbuf", [128, 128], "float32"),
     "ni": ("sbuf", [128, A], "int32"), "nj": ("sbuf", [128, A], "int32"),
 })
-for _n in ("ha", "sen", "ids", "id1", "id2", "kz"):
+for _n in ("ha", "ids", "id1", "id2", "kz"):
     SCRATCH[_n] = ("sbuf", [128, A], "bfloat16")
 for _n in ("xb", "xu", "kc"):
     SCRATCH[_n] = ("sbuf", [128, A], "float32")
@@ -61,7 +63,7 @@ for _e in range(2):
 for _r in range(3):
     SCRATCH["u%d" % _r] = ("sbuf", [128, 2 * A], "float32")
 
-SEMAPHORES = ["cv", "ca", "ct", "cg", "sent", "upr"] + ["d%d" % _n for _n in range(90)] + \
+SEMAPHORES = ["cv", "ca", "ct", "cg", "sent", "upr", "s00"] + ["d%d" % _n for _n in range(90)] + \
     ["m%d%d" % (_e, _r) for _e in range(2) for _r in range(3)]
 
 
@@ -93,7 +95,7 @@ def calls(g, T, topo, r):
                 for name, a, b, rows in x[1]:
                     w = wr
                     if name.startswith("ps"):
-                        a, b, w = 0, 512, not adds
+                        a, b, w = a // 512 * 512, -(-b // 512) * 512, not adds
                     keep = []
                     for (a2, b2, rows2, w2, j) in acc.get(name, []):
                         hit = a < b2 and a2 < b and (rows is None or rows2 is None or rows == rows2)
@@ -105,11 +107,14 @@ def calls(g, T, topo, r):
         ops.append({"q": q, "fn": fn, "deps": deps, "sem": sem, "n": n, "cost": cost, "lat": lat, "after": set(), "wire": wire, "lands": lands})
         return me
 
+    def val(x):
+        return x[0] if isinstance(x, tuple) else x
+
     def cyc(o, a, per):
         return 0.06 + CY * max(64, o[2] * (GAM if len(a[1]) > 1 else per))
 
     def dma(q, out, in_):
-        k = ndma[0]
+        k = ndma[0] if out[1] else 89
         ndma[0] += 1
         e = g.sync if q == "s" else g.scalar
         side = out if out[1] else in_
@@ -123,12 +128,10 @@ def calls(g, T, topo, r):
         return op("v", lambda: g.vector.tensor_tensor(o[0], a[0], b[0], alu), [o], [a, b], cyc(o, a, 1 if a[1][0][0].startswith("ps") else 2))
 
     def ts(o, a, s1, s2, o0, o1=None):
-        v1 = s1[0] if isinstance(s1, tuple) else s1
-        v2 = s2[0] if isinstance(s2, tuple) else s2
         c = cyc(o, a, 0.5 if size(o) + size(a) == 4 else 1)
         if o1 is None:
-            return op("v", lambda: g.vector.tensor_scalar(o[0], a[0], v1, None, o0), [o], [a, s1], c)
-        return op("v", lambda: g.vector.tensor_scalar(o[0], a[0], v1, v2, o0, o1), [o], [a, s1, s2], c)
+            return op("v", lambda: g.vector.tensor_scalar(o[0], a[0], val(s1), None, o0), [o], [a, s1], c)
+        return op("v", lambda: g.vector.tensor_scalar(o[0], a[0], val(s1), val(s2), o0, o1), [o], [a, s1, s2], c)
 
     def cp(o, a):
         return op("v", lambda: g.vector.tensor_copy(o[0], a[0]), [o], [a], cyc(o, a, 0.5 if size(o) + size(a) == 4 else 1))
@@ -137,8 +140,7 @@ def calls(g, T, topo, r):
         return op("v", lambda: g.vector.memset(o[0], c), [o], [], cyc(o, o, size(o) / 4))
 
     def act(o, a, f=ACT.Identity, bias=0.0, scale=1.0):
-        sv = scale[0] if isinstance(scale, tuple) else scale
-        return op("a", lambda: g.scalar.activation(o[0], a[0], f, bias=bias, scale=sv), [o], [a, scale], 0.02 + cyc(o, a, 1))
+        return op("a", lambda: g.scalar.activation(o[0], a[0], f, bias=val(bias), scale=val(scale)), [o], [a, scale, bias], 0.02 + cyc(o, a, 1))
 
     def gcp(o, a):
         return op("g", lambda: g.affine_select(o[0], a[0], [[1, o[2]]], ALU.is_ge, 0.0, 0, 0), [o], [a], 0.17 + 2 * CY * o[2])
@@ -157,136 +159,116 @@ def calls(g, T, topo, r):
         return op("t", fn, [o for o, l, x in items], [y for o, l, x in items for y in (l, x)],
                   sum(0.01 + CY / 2 * max(min(64, l[2]), x[2]) * size(x) ** 2 / 4 for o, l, x in items), adds=not (start or stop))
 
-    def wrap(bank, c0, n, src, col, base, start=True, stop=True):
+    def wrap(bank, n, src, col, base):
         for q in range(0, 16, 4):
-            mms([(X(bank, c0, c0 + n), X(base, 15 - i, 143 - i), X(src, col + i, col + 16 * n, 16)) for i in range(q, q + 4)], start and q == 0, stop and q == 12)
+            mms([(X(bank, 0, n), X(base, 15 - i, 143 - i), X(src, col + i, col + 16 * n, 16)) for i in range(q, q + 4)], q == 0, q == 12)
 
-    def turn(bank, c0, part, src, col, sel, stop):
+    def turn(bank, c0, part, src, col, sel):
         a, b = XP[part]
-        c0 += 128 * part
         for q in range(0, 16, 8):
-            mms([(X(bank, c0 + i, c0 + 128, 16, top=(b - a) // 16), X(src, col + a + i, col + b, 16), X(sel)) for i in range(q, q + 8)], False, stop and q == 8)
+            mms([(X(bank, c0 + i, c0 + 128, 16, top=(b - a) // 16), X(src, col + a + i, col + b, 16), X(sel)) for i in range(q, q + 8)], False, False)
+
+    def terms(items, start, stop, a0, b0, shift=0):
+        cut = [a0] + [c + shift for c in range(512, V, 512) if a0 < c + shift < b0] + [b0]
+        for a, b in zip(cut, cut[1:]):
+            mms([(X("psW", a - shift, b - shift), X(l), X(x, a, b)) for l, x in items], start, stop)
 
     def later(k):
         return list(range(k + 1, NR))
 
-    def engines(k, dsts, part):
+    def engines(k, dsts):
         es = [e for e in topo.engines(T.cores[k], T.cores[dsts[0]]) if all(e in topo.engines(T.cores[k], T.cores[x]) for x in dsts)]
-        return es if part is None else es[part * len(es) // 2:(part + 1) * len(es) // 2]
+        return es if k else es[:len(es) // 2]
 
-    def part_of(k):
-        return 0 if k == 0 else None
-
-    def send(src, land, part, dsts, lat):
+    def send(src, land, dsts, lat, dst=None):
         ids = [DstId(rid=topo.addr(T.cores[k])[0], pnc=topo.addr(T.cores[k])[1]) for k in dsts]
-        es = engines(r, dsts, part)
+        es = engines(r, dsts)
         sent[0] += len(es)
         tr = RemoteDMATransfer(dst_ids=ids, dma_engine_mask=sum(1 << e for e in es), remote_sem=T.sem[land],
-                               srcs=[src[0]], dsts=[X(land, 0, src[2])[0] for _ in dsts])
+                               srcs=[src[0]], dsts=[(dst or src)[0] for _ in dsts])
         return op("g", lambda: g.remote_dma_fused([tr], local_sem=T.sem.sent), [], [src], 0.8 if sent[0] > len(es) else 3.0, lat, sem="",
                   lands=[(k, land) for k in dsts])
 
-    def arrive(name, frm, dsts, part):
-        return op("x", None, [X(name)], [], 0.0, sem=name, n=len(engines(frm, dsts, part)))
-
-    BK = [(512 * j, 512 * j + 512) for j in range(5)]
-    BN = [(max(a, A), b) for a, b in BK]
-    WB = ["psW%d" % j for j in range(5)]
-    XB3 = ["psXA", "psXB", "psXC"]
-    PT = [(A, 1024), (1024, V)]
-    XP = [(A, XS), (XS, V)]
-    KB = {0: ("psXA", 0), 1: ("psXA", 256), 2: ("psXB", 0), 3: ("psXB", 256), 4: ("psXC", 0)}
-    sends = r < NR - 1
+    def arrive(x, name, frm, dsts):
+        return op("x", None, [x], [], 0.0, sem=name, n=len(engines(frm, dsts)))
 
     def kf(j):
         return X("kf", j, j + 1)
 
-    def mklist(k, part, src):
-        a, b = PT[part]
-        wrap(XB3[part], 0, (b - a) // 16, src, a, "BE")
-        cp(lst(k, a, b), X(XB3[part], 0, (b - a) // 16))
-
     def lst(k, a, b):
         return X("L%d" % k, a // 16, b // 16)
 
-    def nbl(k, a=A, b=V):
+    def nbl(k, a, b):
         return X("nbl", k * NW + a // 16, k * NW + b // 16)
 
-    def twin(dst, src, a, b, on_g):
-        if on_g:
-            gcp(X(dst, a, b), X(src, a, b))
-        else:
-            dma("s", X(dst, a, b), X(src, a, b))
+    def mklist(k, bank, src, a, b):
+        wrap(bank, (b - a) // 16, src, a, "BE")
+        return cp(lst(k, a, b), X(bank, 0, (b - a) // 16))
 
-    def wb(j, a, b):
-        return X(WB[j], a - BK[j][0], b - BK[j][0]) if j < 5 else X("psXC", 0, b - a)
+    def twin(dst, src, a, b, j):
+        return gcp(X(dst, a, b), X(src, a, b)) if j in ON_G else dma("s", X(dst, a, b), X(src, a, b))
 
-    def terms(j, items, start, stop, a, b):
-        return mms([(wb(j, a, b), X(l), X(x, a, b)) for l, x in items], start, stop)
-
-    def pieces(a, b, most=PIECE):
+    def pieces(a, b, most):
         n = -((a - b) // most)
         cut = [a + (b - a) * i // n // 32 * 32 for i in range(n)] + [b]
         return list(zip(cut, cut[1:]))
 
-    def halves(a, b):
-        return pieces(a, b, 1400)
+    def line(*lists):
+        seq = [x[n] for n in range(max(map(len, lists))) for x in lists if n < len(x)]
+        for a, b in zip(seq, seq[1:]):
+            ops[b]["after"].add(a)
+        return seq
 
-    def way_at(ways, a):
-        return [way for way, b in ways if a < b][0]
-
-    RB = pieces(A, V, (V - A) // NB + 32)
-    LB = BN
+    XB3 = ["psXA", "psXB", "psXC"]
+    RB = pieces(A, V, (V - A) // 5 + 32)
+    BN = [(max(A, 512 * j), 512 * j + 512) for j in range(5)]
+    sends = r < NR - 1
 
     dma("s", X("pb"), dram(T.par[:]))
-    counts = [iota("ki", [[0, 1]], 1, 1), iota("xi", [[1, 144]]), iota("xg", [[16, 8]]), iota("cc", [[16, NW]])]
+    counts = [iota("ki", [[0, 1]], 1, 1), iota("xi", [[1, 144]]), iota("xg", [[16, 8]]), iota("cc", [[1, NW]])]
     if r > 0:
         dma("a", X("upi"), dram(T.up[:]))
-        counts.append(send(X("upi"), "upr", None, [r - 1], 8.0))
+        counts.append(send(X("upi"), "upr", [r - 1], 8.0, X("upr")))
         ops[counts[-1]]["after"].update(counts[:-1])
     dma("a", X("ha"), dram(T.hf[:, 0:A]))
     dma("s", X("h", A, HS), dram(T.hf[:, A:HS]))
-    ops[iota("ck", [[1, 5], [0, 256]])]["after"].update(counts)
+    ops[iota("ck", [[NW, 5], [0, 128]])]["after"].update(counts)
     fill(X("C0", A, V), 0.0)
     ts(X("kj", 0, 1), X("ki", 0, 1), 15, None, ALU.bitwise_and)
     ts(X("kj", 1, 2), X("ki", 0, 1), 112, None, ALU.bitwise_and)
     cp(kf(0), X("ki", 0, 1))
     cp(X("kf", 1, 3), X("kj", 0, 2))
-    ts(kf(10), kf(2), 15.0, None, ALU.add)
-    ts(kf(5), kf(1), 0.0, None, ALU.is_equal)
-    ts(kf(6), kf(1), 1.0, None, ALU.is_equal)
-    ts(kf(7), kf(1), 2.0, None, ALU.is_equal)
-    ts(kf(4), kf(6), kf(7), None, ALU.add)
-    ts(kf(8), kf(5), -0.75, 1.0, ALU.mult, ALU.add)
-    ts(kf(9), kf(5), 1.0, None, ALU.add)
+    ts(X("kf", 5, 8), X("xi", 0, 3), kf(1), None, ALU.is_equal)
+    act(kf(4), kf(6), bias=kf(7))
+    act(kf(8), kf(5), bias=1.0, scale=-0.75)
+    act(kf(9), kf(5), bias=1.0)
+    act(kf(10), kf(6), scale=float(V))
     ts(X("hl", 0, NW), X("pb"), 8.0, 0.0, ALU.subtract, ALU.max)
     tt(X("hl", NW, 2 * NW), X("pb"), X("hl", 0, NW), ALU.subtract)
     first = [dma("s", X("C0", 0, V, rows=1), X("hl", 0, NW)), dma("s", X("C0", 0, V, rows=2), X("hl", NW, 2 * NW))]
     first.append(dma("s", X("h", HS, V), dram(T.hf[:, HS:V])))
     ops[first[2]]["deps"].update(ops[first[1]]["deps"])
-    ops[first[2]]["after"].update(ops[first[1]]["deps"])
     late = {}
-    for k, name, src in ((0, "b", T.bt), (1, "d", T.dr), (2, "nbi", T.nb)):
+    for name, src in (("b", T.bt), ("d", T.dr), ("nbi", T.nb)):
         n = T[name].shape[1] // 2
-        late[k] = [dma("s", X(name, a, a + n), dram(src[:, a:a + n])) for a in (0, n)]
-        ops[late[k][0]]["after"].update(first)
-    ops[dma("s", X("dq"), dram(T.dr[0:128:16, :]))]["after"].update(late[1])
+        late[name] = [dma("s", X(name, a, a + n), dram(src[:, a:a + n])) for a in (0, n)]
+        ops[late[name][0]]["after"].update(first)
+    ops[dma("s", X("dq"), dram(T.dr[0:128:16, :]))]["after"].update(late["d"])
     ts(X("I1"), X("xi", 0, 128), kf(0), None, ALU.is_equal)
-    for name, w in (("BE", kf(4)), ("BG", kf(6))):
-        ts(X(name), X("xi"), kf(10), w, ALU.is_equal, ALU.mult)
-    ts(X("G8"), X("xg"), kf(2), 8.0, ALU.is_equal, ALU.mult)
-    ts(X("GF"), X("xg"), kf(2), kf(5), ALU.is_equal, ALU.mult)
-    for name, src, w in (("I256", "I1", 256.0), ("I2", "I1", 2.0), ("Im1", "I1", -1.0), ("I512", "I1", 512.0), ("I1024", "I1", 1024.0),
-                         ("I32", "I1", 1.0), ("IV", "I1", float(V)), ("G16", "G8", 2.0), ("Gm8", "G8", -1.0), ("GFm", "GF", -1.0)):
+    ts(X("BD"), X("xi"), 15.0, kf(2), ALU.subtract, ALU.is_equal)
+    ts(X("G1"), X("xg"), kf(2), None, ALU.is_equal)
+    for name, src, w in (("BE", "BD", kf(4)), ("BG", "BD", kf(6)), ("GF", "G1", kf(5)),
+                         ("I256", "I1", 256.0), ("I2", "I1", 2.0), ("Im1", "I1", -1.0), ("I512", "I1", 512.0), ("I1024", "I1", 1024.0),
+                         ("I32", "I1", 1.0), ("Gk", "G1", 1024.0), ("G2k", "G1", 2048.0), ("Gmk", "G1", -1024.0), ("G8k", "G1", 8192.0), ("GE", "G1", kf(4)),
+                         ("GFm", "GF", -1.0)):
         act(X(name), X(src), scale=w)
-    ts(X("id1"), X("xi", 0, A), kf(6), 1.0, ALU.mult, ALU.add)
-    ts(X("id2"), X("xi", 0, A), kf(6), kf(9), ALU.mult, ALU.add)
+    act(X("id1"), X("xi", 0, A), bias=1.0, scale=kf(6))
+    act(X("id2"), X("xi", 0, A), bias=kf(9), scale=kf(6))
     act(X("ids"), X("xi", 0, A), scale=kf(7))
-    ts(X("sen"), X("xi", 0, A), -1.0, kf(6), ALU.is_gt, ALU.mult)
     for name in ("C0", "C1", "T1", "T2"):
-        act(X(name, 0, A), X("sen"), scale=float(V))
+        act(X(name, 0, A), X("xi", 0, A), bias=kf(10), scale=0.0)
     for name in ("T1", "T2"):
-        act(X(name, V, W), X("sen", 0, 16), scale=float(V))
+        act(X(name, V, W), X("xi", 0, 16), bias=kf(10), scale=0.0)
     tt(X("h", 0, A), X("id2"), X("ha"), ALU.mult)
     tt(X("P1", 0, A), X("id1"), X("ha"), ALU.mult)
     gcp(X("P0", 0, A), X("P1", 0, A))
@@ -295,24 +277,25 @@ def calls(g, T, topo, r):
     for name in ("S0", "S1"):
         gcp(X(name, 0, A), X("b", 0, A))
         act(X(name, V, W), X("xi", 0, 16), scale=0.0)
-    for name in ("L0", "idx"):
-        ts(X(name, 0, C0), X("cc", 0, C0), kf(1), None, ALU.add)
+    spare = [ts(X(name, 0, C0), X("cc", 0, C0), 16.0, kf(1), ALU.mult, ALU.add) for name in ("L0", "idx")]
     if r == 0:
         fill(X("u0", 0, A), 1.0)
         fill(X("kz"), 0.0)
         fill(X("kc"), CB - 127.5)
-    for part, (a, b) in enumerate([(A, HS), (HS, V)]):
-        mklist(0, part, "C0")
-        ts(X("PD", a, b), X("h", a, b), kf(8), None, ALU.mult)
+    made = {(0, part): mklist(0, XB3[part], "C0", a, b) for part, (a, b) in enumerate(PT)}
+    ts(X("PD", A, HS), X("h", A, HS), kf(8), None, ALU.mult)
+    line([made[0, 0], ts(X("PD", HS, V), X("h", HS, V), kf(8), None, ALU.mult)])
     cp(X("nbl"), X("nbi"))
     if sends:
-        arrive("upr", r + 1, [r], None)
+        arrive(X("upr"), "upr", r + 1, [r])
         cp(X("l8", 0, 4), X("upr"))
-    for a, b in pieces(A, V):
+    for a, b in pieces(A, V, 900):
         act(X("gs", a, b), X("d", a, b), ACT.Sign, bias=127.5, scale=-1.0)
     act(X("dw"), X("dq"), ACT.Sign, bias=127.5, scale=-1.0)
     act(X("dq"), X("dw"), scale=0.25)
     gcp(X("gs", 0, A), X("id2"))
+    act(X("low"), X("ck", 0, 512), bias=-2.0 ** 24, scale=0.0)
+    act(X("tie"), X("ck", 0, 512), bias=4096.0, scale=0.0)
 
     for e in range(2):
         C = "C%d" % e
@@ -322,85 +305,112 @@ def calls(g, T, topo, r):
         mn = "m%d%d" % (e, r)
         uh = X("u0" if r == 0 else "m%d0" % e if r == 1 else "u%d" % (r - 1), 0, A)
 
-        jump = {}
+        block, walks = {}, {}
         for k in range(5):
-            for j, (a, b) in enumerate(RB if k < 4 else LB):
+            for j, (a, b) in enumerate(RB if k < 4 else BN):
                 n = tt(X(PP[k + 1], a, b), G(X(PP[k], 0, V if k == 0 else W), lst(k, a, b)), X("GD" if k == 0 and e == 1 else "PD", a, b), ALU.mult)
+                block[k, j] = n
                 if e == 0 and (k, j) in LATE:
                     ops[late[LATE[k, j][0]][LATE[k, j][1]]]["deps"].add(n)
                 if k < 4:
-                    twin("PD", PP[k + 1], a, b, j in P_ON_G)
+                    twin("PD", PP[k + 1], a, b, j)
             for part, (a, b) in enumerate(PT if k < 4 else []):
-                jump[k, part] = act(X(TT[k + 1], a, b), G(X(TT[k], 0, V if k == 0 else W), lst(k, a, b)))
-                mklist(k + 1, part, TT[k + 1])
+                jump = act(X(TT[k + 1], a, b), G(X(TT[k], 0, V if k == 0 else W), lst(k, a, b)))
+                made[k + 1, part] = mklist(k + 1, XB3[part], TT[k + 1], a, b)
             if sends and 1 <= k < 4:
                 n = 2 << k
                 act(X("tu", 16 * n, 32 * n), G(X(TT[k + 1]), X("l8", 0, n)))
-                wrap("psXC", 0, n, "tu", 16 * n, "BE")
-                cp(X("l8", n, 2 * n), X("psXC", 0, n))
+                wrap("psXC", n, "tu", 16 * n, "BE")
+                walks[k] = cp(X("l8", n, 2 * n), X("psXC", 0, n))
         gcp(X(C, 0, A), X("ids"))
         if e == 1:
-            for a, b in PT:
-                tt(X("D1", a, b), G(X("Hh"), lst(0, a, b)), X("d", a, b), ALU.mult)
-            for a, b in BN:
+            spare = [tt(X("D1", a, b), G(X("Hh"), lst(0, a, b)), X("d", a, b), ALU.mult) for a, b in NEW[:2] + [(XS, 2336), (2336, V)]]
+            for a, b in EV:
                 act(X("Zp", a, b), G(X("Z"), lst(0, a, b)))
-        for j, (a, b) in enumerate(LB):
+        for j, (a, b) in enumerate(EV):
             if e == 0:
-                terms(j, [("I1", "b"), ("I256", "h")], True, True, a, b)
-                act(X("U0", a, b), wb(j, a, b), ACT.Relu, bias=-256.0)
-                terms(j, [("I2", "U0"), ("Im1", "b")], True, False, a, b)
+                terms([("I1", "b"), ("I256", "h")], True, True, a, b)
+                act(X("U0", a, b), X("psW", a, b), ACT.Relu, bias=-256.0)
+                terms([("I2", "U0"), ("Im1", "b")], True, False, a, b)
             else:
-                terms(j, [("I1", "Z"), ("I512", "gs")], True, False, a, b)
-                terms(j, [("I2", "D1")], False, False, a, b)
-                terms(j, [("Im1", "Zp")], False, True, a, b)
-                n = act(X("SD", a, b), wb(j, a, b), ACT.Abs)
-                if j in AHEAD:
-                    ops[jump[AHEAD[j]]]["after"].add(n)
-                terms(j, [("I32", "SD")], True, False, a, b)
-            ts(X("s", a if j else 0, b), X(PP[5], a if j else 0, b), 0.0, 0.5, ALU.is_gt, ALU.subtract)
-            terms(j, [("I512" if e == 0 else "I1024", "s")], False, True, a, b)
-            act(X("S0", a, b), wb(j, a, b), ACT.Abs, bias=0.0 if e == 0 else -512.0)
+                terms([("I1", "Z"), ("I512", "gs")], True, False, a, b)
+                terms([("I2", "D1")], False, False, a, b)
+                terms([("Im1", "Zp")], False, True, a, b)
+                n = act(X("SD", a, b), X("psW", a, b), ACT.Abs)
+                if j < 2:
+                    ops[jump]["after"].add(n)
+                terms([("I32", "SD")], True, False, a, b)
+        for j, (a, b) in enumerate(BN):
+            block["s", j] = ts(X("s", a if j else 0, b), X(PP[5], a if j else 0, b), 0.0, 0.5, ALU.is_gt, ALU.subtract)
+            terms([("I512" if e == 0 else "I1024", "s")], False, True, a, b)
+            steps = act(X("S0", a, b), X("psW", a, b), ACT.Abs, bias=0.0 if e == 0 else -512.0)
+        seq = []
+        for k in range(5):
+            B = [block[k, j] for j in range(5)]
+            seq += B[:1] + ([made[k, 1]] if k or not e else [])
+            if k < 4:
+                seq += B[1:4] + ([made[k + 1, 0]] if k or not e else []) + B[4:]
+                seq += ([spare[0], made[1, 0], spare[1]], spare[2:3], spare[3:], [])[k] if e else spare[k:k + 1]
+                seq += [walks[k - 1]] if k - 1 in walks else []
+            else:
+                seq += [n for j in range(1, 5) for n in (B[j], block["s", j - 1])] + [block["s", 4]]
+        line(seq)
         for j, (a, b) in enumerate(RB):
-            twin("SD", "S0", a, b, j in S_ON_G)
-        dma("a", X(C, 0, V, rows=0), X(PP[5], 0, V, rows=0))
+            twin("SD", "S0", a, b, j)
+        for a, b in ((0, 2048), (2048, V)):
+            dma("s", X(C, a, b, rows=0), X(PP[5], a, b, rows=0))
         if sends:
-            act(X("tu", 0, A), G(X(PP[5], 0, V), X("l8", 0, 4)))
+            ops[act(X("tu", 0, A), G(X(PP[5], 0, V), X("l8", 0, 4)))]["after"].add(steps)
             act(X(mn, 0, A), X("tu", 0, A), ACT.Sign)
+            if r == e == 0:
+                send(X(mn, 0, A), "s00", later(0), 8.0)
             if r > 0:
-                wrap("psXC", 0, 4, "tu", 0, "BG")
+                wrap("psXC", 4, "tu", 0, "BG")
                 act(X(mn, 2 * A, 2 * A + 4), X("psXC", 0, 4), ACT.Abs)
                 act(X(mn, 2 * A + 4, MW), X("psXC", 0, 4), ACT.Abs)
-        wrap("psXA", 0, NW, PP[5], 0, "BG")
+        wrap("psXA", NW, PP[5], 0, "BG")
         act(X("an"), X("psXA", 0, NW), ACT.Abs)
-        ts(X("L5"), X("an"), 1.0, None, ALU.subtract)
-        mms([(X("psXB", 0, 256), X("I1"), X("ck", 0, 256))], True, False)
-        for part in (1, 0):
-            turn("psXB", 0, part, PP[5], 0, "GF", part == 0)
+        anchors = ts(X("L5"), X("an"), 1.0, None, ALU.subtract)
+        mms([(X("psXB", c, c + 128), X("I1"), X("ck", 0, 128)) for c in (0, 128)], True, False)
+        for part in range(2):
+            turn("psXB", 128 * part, part, PP[5], 0, "GF")
+        mms([(X("psXB", 0, A), X("I1"), X("ck", 0, A))], False, True)
         act(X("av"), X("psXB", 0, 256), ACT.Abs)
 
+        cands = []
         for k in range(4):
             bank = XB3[(k + 2) % 3]
             mms([(X(bank, 0, 256), X("I1"), X("av"))], True, False)
-            for a, b in pieces(A, V):
-                act(X(C, (k + 1) * V + a, (k + 1) * V + b), G(X(C, 0, V), nbl(k, a, b)), ACT.Abs)
-            for part in (1, 0):
-                turn(bank, 0, part, C, (k + 1) * V, "GFm", part == 0)
+            for a, b in pieces(A, V, 900):
+                cands.append(act(X(C, (k + 1) * V + a, (k + 1) * V + b), G(X(C, 0, V), nbl(k, a, b)), ACT.Abs))
+            n0 = len(ops)
+            for part in range(2):
+                turn(bank, 128 * part, part, C, (k + 1) * V, "GFm")
+            mms([(X(bank, 0, A), X("I1"), X("ck", 0, A))], False, True)
+            pens = range(n0, len(ops))
             act(X("pen", k * 256, k * 256 + 256), X(bank, 0, 256), ACT.Relu, scale=2.0 ** 60)
 
+        sums = {}
         for k in range(5):
             for j, (a, b) in enumerate(RB if k < 4 else BN):
-                tt(X(SS[k + 1], a, b), G(X(SS[k]), lst(k, a, b)), X("SD", a, b), ALU.add)
+                sums[k, j] = tt(X(SS[k + 1], a, b), G(X(SS[k]), lst(k, a, b)), X("SD", a, b), ALU.add)
                 if k < 4:
-                    twin("SD", SS[k + 1], a, b, j in S_ON_G)
+                    n = twin("SD", SS[k + 1], a, b, 1 if sends and (k, j) == (2, 2) else j)
+                    if sends and j in ON_G and (k, j) > (2, 2):
+                        ops[n]["after"].add(out)
             if k == 1 and sends:
-                act(X("z8"), G(X(SS[2]), X("l8")))
-                mms([(X("psW0", 0, A), X("I32"), X("z8", A * q, A * q + A)) for q in range(8)], True, True)
-                act(X(mn, A, 2 * A), X("psW0", 0, A))
-                send(X(mn, 0, MW if r > 0 else 2 * A), mn, part_of(r), later(r), 3.0)
+                far = act(X("z8"), G(X(SS[2]), X("l8")))
+                mms([(X("psW", 0, A), X("I32"), X("z8", A * q, A * q + A)) for q in range(8)], True, True)
+                line([far, cands[6], act(X(mn, A, 2 * A), X("psW", 0, A))] + cands[7:])
+                out = send(X(mn, A if r == e == 0 else 0, MW if r > 0 else 2 * A), mn, later(r), 2.0)
+        k = 0 if e or not sends else 1
+        line([sums[k, 4], anchors, sums[k + 1, 0]])
         if r > 0:
+            if e == 0:
+                arrive(X("m00", 0, A), "s00", 0, later(0))
             for k in range(r):
-                arrive("m%d%d" % (e, k), k, later(k), part_of(k))
-            cur = "m%d0" % e
+                arrive(X("m%d%d" % (e, k), A if k == e == 0 else 0), "m%d%d" % (e, k), k, later(k))
+            cur, n0 = "m%d0" % e, len(ops)
             if r == 1:
                 cp(X("ni"), X(cur, A, 2 * A))
             for k in range(1, r):
@@ -413,15 +423,22 @@ def calls(g, T, topo, r):
             ts(X("nj"), X("ni"), 255, None, ALU.bitwise_and)
             tt(X("kz"), X("nj"), uh, ALU.mult)
             tt(X("kc"), X("kz"), X("xu"), ALU.add)
-        for a, b in BK:
-            (act if a < KS[e] else cp)(X("D0", a, b), G(X("kz"), lst(5, a, b)))
-        for j, (a, b) in enumerate(LB):
+            s = [n for n in range(n0, len(ops)) if ops[n]["q"] == "v"]
+            slots = {1: [[], [], s[:1]], 2: [s[:1], s[1:2], s[2:3]], 3: [s[0:4:3], s[1:2], s[2:5:2], s[5:6]]}[r] + [s[-3:-1], s[-1:], []]
+            line([n for x, slot in zip(sorted(sums)[17:], slots) for n in [sums[x]] + slot])
+        rounded = []
+        for j, (a, b) in enumerate(BN):
             a = a if j else 0
-            terms(j, [("I32", "S1")], True, False, a, b)
-            terms(j, [("I1", "D0")], False, False, a, b)
-            tt(X("tb", a, b), G(X("kc"), lst(5, a, b)), X("S1", a, b), ALU.add)
-            terms(j, [("Im1", "tb")], False, True, a, b)
-            placed = act(X("Z", a, b), wb(j, a, b), ACT.Abs, bias=CB)
+            act(X("D0", a, b), G(X("kz"), lst(5, a, b)))
+            terms([("I32", "S1")], True, False, a, b)
+            terms([("I1", "D0")], False, False, a, b)
+            rounded.append(tt(X("tb", a, b), G(X("kc"), lst(5, a, b)), X("S1", a, b), ALU.add))
+            terms([("Im1", "tb")], False, True, a, b)
+            placed = act(X("Z", a, b), X("psW", a, b), ACT.Abs, bias=CB)
+        line(rounded)
+        for n in pens:
+            ops[n]["after"].add(placed - 1)
+        ops[rounded[0]]["after"].update(sums.values())
         if e == 1:
             dma("s", dram(T.yx[:]), X("Z"))
         else:
@@ -432,73 +449,92 @@ def calls(g, T, topo, r):
                 gcp(X(name, 0, A), X("id1"))
             for name in ("S0", "S1"):
                 gcp(X(name, 0, A), X("xb"))
-            for a, b in BK:
-                tt(X("Hh", a, b), G(uh, lst(5, a, b)), X("s", a, b), ALU.mult)
+            signs = [tt(X("Hh", a, b), G(uh, lst(5, a, b)), X("s", a, b), ALU.mult) for a, b in pieces(0, V, 384)]
 
-        for k in (0, 2, 4):
-            n = min(512, (5 - k) * 256)
-            mms([(X(KB[k][0], 0, n), X("I1"), X("ck", k * 256, k * 256 + n))], True, False)
-        left = {bank: 0 for bank in XB3}
-        plan = list(enumerate([[("s", V)]] + VOTES[e]))
-        for k, ways in plan:
-            left[KB[k][0]] += 2 + sum(1 for a, b in XP if way_at(ways, a) == "v")
-
-        def key(k, src, sel, part):
-            left[KB[k][0]] -= 1
-            turn(KB[k][0], KB[k][1], part, src, 0, sel, False)
-            if left[KB[k][0]] == 0:
-                mms([(X(KB[q][0], KB[q][1], KB[q][1] + 256), X("I1"), X("pen", (q - 1) * 256, q * 256))
-                     for q in range(1, 5) if KB[q][0] == KB[k][0]], False, True)
-
-        for a, b in halves(ZS[e], V) if ZS[e] < V else []:
-            cp(X("Zp", a, b), G(X("Z"), lst(0, a, b)))
-        for a, b in halves(0, ZS[e]):
-            act(X("Zp", a, b), G(X("Z"), lst(0, a, b)))
-        for k, ways in plan:
-            D, U, a0, todo = "D%d" % (k - 1), "U%d" % k, A, [0, 1]
-            for way, b0 in ways:
-                cuts = [(a0, XS), (XS, b0)] if a0 < XS < b0 else [(a0, b0)]
-                for a, b in [x for c in cuts for x in halves(*c)]:
-                    if way != "s":
-                        tt(X(D, a, b), G(X("Zp"), nbl(k - 1, a, b)), X("Z", a, b), ALU.subtract)
-                    elif k > 0:
-                        act(X(D, a, b), G(X("Zp"), nbl(k - 1, a, b)))
-                    if way == "b":
-                        act(X(U, a, b), X(D, a, b), ACT.Abs)
-                for a, b in cuts if way == "v" else []:
-                    key(k, D, "Gm8", XP.index((a, b)))
-                    ts(X(U, a, b), X(D, a, b), 0.0, None, ALU.max)
-                for j in range(5) if way == "s" else []:
-                    a, b = max(a0, BK[j][0]), min(b0, BK[j][1])
-                    if a < b:
-                        terms(j, [("Im1", "Z")], True, False, a, b)
-                        terms(j, [("I1", D if k > 0 else "Zp")], False, True, a, b)
-                        act(X(U, a, b), wb(j, a, b), ACT.Abs)
-                while todo and XP[todo[0]][1] <= b0:
-                    part = todo.pop(0)
-                    key(k, U, "G16" if way_at(ways, XP[part][0]) == "v" else "G8", part)
-                a0 = b0
-        act(X("best"), X("psXA", 0, 256))
-        mms([(X("psW4", C0, NW), X("I1"), X("cc", C0, NW))], True, False)
-        for k in range(1, 5):
-            tt(X("best" if k < 4 else "bi"), X(KB[k][0], KB[k][1], KB[k][1] + 256), X("best"), ALU.min)
-        ts(X("bj"), X("bi"), 7, None, ALU.bitwise_and)
-        cp(X("kb"), X("bj"))
-        mms([(X("psW4", C0, C0 + 128), X("kb", 0, 128), X("IV")),
-             (X("psW4", C0 + 128, NW), X("kb", 128, 256, top=XN), X("IV", 0, XN, top=XN))], False, True)
-        ts(X("idx", C0, NW), X("psW4", C0, NW), kf(1), None, ALU.add)
+        cp(X("Zp", ZS, V), G(X("Z"), lst(0, ZS, V)))
+        act(X("Zp", 0, ZS), G(X("Z"), lst(0, 0, ZS)))
+        gathers, work, chain = [[], []], [[], []], [[], []]
+        for part, (a1, b1) in enumerate(XP):
+            four, fifth = (("psXA", "psXB"), ("psXC", "psW"))[part]
+            c1, n1, back = 128 * part, (b1 - a1) // 16, 512 + 512 * part
+            whole = e == part == 1
+            mms([(X(four), X("I1"), X("low" if whole else "ck", 0, 512))] + [(X(four, 128, 512), X("I1"), X("tie", 0, 384))] * whole, True, False)
+            for k, ways in enumerate([[("s", V)]] + VOTES):
+                if whole and ways[0][0] == "v":
+                    ways = [("b", V)]
+                D, U, a0 = "D%d" % (k - 1), "U%d" % k, a1
+                bank, c0 = (four, 128 * k) if k < 4 else (fifth, 0)
+                if k == 4:
+                    mms([(X(fifth, 0, 128), X("I1"), x) for x in ([X("low", 0, 128), X("tie", 0, 128)] if whole else [X("ck", 512, 640)])], True, False)
+                if whole:
+                    turn(bank, c0, part, C, k * V, "GE")
+                for way, b0 in ways:
+                    b0 = min(b0, b1)
+                    if b0 <= a0:
+                        continue
+                    for a, b in pieces(a0, b0, 1400):
+                        if way != "s":
+                            work[part].append(tt(X(D, a, b), G(X("Zp"), nbl(k - 1, a, b)), X("Z", a, b), ALU.subtract))
+                            gathers[part].append(work[part][-1])
+                        elif k > 0:
+                            gathers[part].append(act(X(D, a, b), G(X("Zp"), nbl(k - 1, a, b))))
+                        if way == "b":
+                            act(X(U, a, b), X(D, a, b), ACT.Abs)
+                    if way == "v":
+                        turn(bank, c0, part, D, 0, "Gmk")
+                        work[part].append(ts(X(U, a0, b0), X(D, a0, b0), 0.0, None, ALU.max))
+                    for a, b in [(a, min(a + 1024, b0)) for a in range(a0, b0, 1024)] if way == "s" else []:
+                        terms([("Im1", "Z")], True, False, a, b, A)
+                        terms([("I1", D if k > 0 else "Zp")], False, True, a, b, A)
+                        act(X(U, a, b), X("psW", a - A, b - A), ACT.Abs)
+                    a0 = b0
+                turn(bank, c0, part, U, 0, "G8k" if whole else "G2k" if ways[0][0] == "v" else "Gk")
+                if k >= 3:
+                    mms([(X(bank, 128 * q % 512, 128 * q % 512 + 128), X("I1"), X("pen", 256 * q - 256 + c1, 256 * q - 128 + c1))
+                         for q in ((1, 2, 3) if k == 3 else (4,))], False, True)
+            act(X("best", c1, c1 + 128), X(four, 0, 128))
+            for k in range(1, 5) if whole else []:
+                chain[part].append(tt(X("bi", c1, c1 + 128), X(four, 128 * k, 128 * k + 128) if k < 4 else X(fifth, 0, 128),
+                                      X("bj" if k > 1 else "best", c1, c1 + 128), ALU.min))
+                chain[part].append(ts(X("bj", c1, c1 + 128), X("bi", c1, c1 + 128), -4097 if k < 4 else 4095, None, ALU.bitwise_and))
+            if whole:
+                chain[part].append(cp(X("pf"), X("bj", c1, c1 + 128)))
+                for q in range(8):
+                    dma("sa"[q % 2], dram(T.yp[q, XS:V]), X("pf", 16 * q, 16 * q + 16, top=n1))
+                continue
+            for k in range(1, 5):
+                chain[part].append(tt(X("best" if k < 4 else "bi", c1, c1 + 128), X(four, 128 * k, 128 * k + 128) if k < 4 else X(fifth, 0, 128),
+                                      X("best", c1, c1 + 128), ALU.min))
+            chain[part].append(ts(X("bj", c1, c1 + 128), X("bi", c1, c1 + 128), 1023, None, ALU.bitwise_and))
+            chain[part].append(cp(X("kb", c1, c1 + 128), X("bj", c1, c1 + 128)))
+            o = X("psW", back, back + n1)
+            mms([(o, X("I1"), X("cc", a1 // 16, b1 // 16))], True, False)
+            mms([(o, X("kb", c1, c1 + 128, top=n1), X("I1", 0, n1, top=n1))], False, True)
+            chain[part].append(ts(X("idx", a1 // 16, b1 // 16), o, 16.0, kf(1), ALU.mult, ALU.add))
+        for n in gathers[1]:
+            ops[n]["after"].update(gathers[0])
+        ops[line(chain[0][:6], work[1][2:])[0]]["after"].update(work[0] + work[1][:2])
+        one = line([chain[0][5], signs[3] if e == 0 else chain[1][0], chain[0][6]])
         if e == 0:
-            cp(X("C1", A, CS0), G(X(C), X("idx", A // 16, CS0 // 16)))
-            for part, (a, b) in enumerate(PT):
-                act(X("C1", max(a, CS0), b), G(X(C), X("idx", max(a, CS0) // 16, b // 16)))
-                mklist(0, part, "C1")
+            two = line(chain[1], signs[4:])
+            for n, (a, b) in enumerate(NEW):
+                act(X("C1", a, b), G(X(C), X("idx", a // 16, b // 16)))
+                mklist(0, XB3[n], "C1", a, b)
         else:
-            for q, (a, b) in enumerate(OUT):
-                (cp if q % 2 == 0 else act)(X("T2", a, b), G(X(C), X("idx", a // 16, b // 16)))
-                mms([(X("psXA", 0, NW), X("BE", 15 - i, 143 - i), X("T2", NW * i, NW * i + NW)) for i in range(a // NW, b // NW)], q == 0, b == V)
-            cp(X("po"), X("psXA", 0, NW))
-            dma("s", dram(T.yp[:]), X("po"))
+            outs = []
+            for a, b, q in OUT:
+                n = (cp if q == "v" else act)(X("T2", a, b), G(X(C), X("idx", a // 16, b // 16)))
+                outs += [n] if q == "v" else []
+                mms([(X("psXA", 0, XW), X("BE", 15 - i, 143 - i), X("T2", XW * i, XW * i + XW)) for i in range(a // XW, b // XW)], a == 0, b == XS)
+            two = line(outs, chain[1][1:])
+            act(X("po", 0, XW), X("psXA", 0, XW))
+            dma("s", dram(T.yp[:, 0:XS]), X("po", 0, XW))
+        ops[two[0]]["after"].add(one[-1])
     return ops, sent[0]
+
+
+def gap(ops, a, b):
+    return 0.0 if ops[a]["q"] == ops[b]["q"] == "t" or a in ops[b]["soft"] or b in ops[a]["soft"] else WAKE
 
 
 def arrange(ops, pre, succ, weight, back):
@@ -518,7 +554,7 @@ def arrange(ops, pre, succ, weight, back):
         for s in succ[j]:
             count[s] -= 1
             if count[s] == 0:
-                ready[s] = ops[s]["lat"] * back + max(done[d] + (0.0 if ops[d]["q"] == ops[s]["q"] == "t" else WAKE) for d in pre[s])
+                ready[s] = ops[s]["lat"] * back + max(done[d] + gap(ops, d, s) for d in pre[s])
     return order, done
 
 
@@ -539,7 +575,7 @@ def place(ops, pre, succ, weight, back):
         j = max(ready, key=lambda x: (weight[x], -x))
         ready.remove(j)
         o = ops[j]
-        t = o["lat"] * back + max([done[d] + (0.0 if ops[d]["q"] == o["q"] == "t" else WAKE) for d in pre[j]], default=0.0)
+        t = o["lat"] * back + max([done[d] + gap(ops, d, j) for d in pre[j]], default=0.0)
         if o["wire"] and back:
             t = fit(o["Q"][0], t, o["wire"]) + o["wire"]
         start[j] = fit(o["Q"], t, o["cost"])
@@ -554,7 +590,7 @@ def place(ops, pre, succ, weight, back):
     return sorted(start, key=lambda x: (start[x], done[x])), done
 
 
-ORDER, RULES = {}, [arrange, arrange, place, place, place]
+ORDER = {}
 
 
 def orders(g, T, topo):
@@ -563,7 +599,7 @@ def orders(g, T, topo):
         for k in range(len(T.cores)):
             base = len(ops)
             for j, o in enumerate(calls(g, T, topo, k)[0]):
-                ops.append(dict(o, Q=(k, o["q"])))
+                ops.append(dict(o, Q=(k, o["q"]), soft={base + d for d in o["after"] - o["deps"]}))
                 pre.append({base + d for d in o["deps"] | o["after"]})
                 home.append((k, j))
         landing = {(o["Q"][0], o["sem"]): j for j, o in enumerate(ops) if o["q"] == "x"}
@@ -575,10 +611,9 @@ def orders(g, T, topo):
             for d in p:
                 succ[d].add(j)
         order, head = arrange(ops, pre, succ, [-j for k, j in home], 0)
-        for rule in RULES:
+        for rule in (arrange, arrange, place, place, place):
             order, tail = rule(ops, succ, pre, head, 1)
             order, head = rule(ops, pre, succ, tail, 0)
-        ORDER["end"] = max(head.values())
         for j in order:
             ORDER.setdefault(home[j][0], []).append(home[j][1])
     return ORDER
@@ -592,14 +627,14 @@ def rank_program(g, core, T, topo):
     ops, sent = calls(g, T, topo, r)
     Q = {"v": g.vector, "a": g.scalar, "t": g.tensor, "g": g, "s": g.sync}
     CS = {"v": "cv", "a": "ca", "t": "ct", "g": "cg"}
-    place = {j: n for n, j in enumerate(order)}
+    at = {j: n for n, j in enumerate(order)}
     need = set()
     for o in ops:
         o["deps"] = {d for d in o["deps"] if not (o["q"] == "t" and ops[d]["q"] == "t")}
         last = {}
         for d in o["deps"]:
             if ops[d]["sem"] is None:
-                last[ops[d]["q"]] = max(last.get(ops[d]["q"], d), d, key=lambda x: place[x])
+                last[ops[d]["q"]] = max(last.get(ops[d]["q"], d), d, key=lambda x: at[x])
         need.update(last.values())
     cnt, mark = {q: 0 for q in CS}, {}
     for j in order:
@@ -627,8 +662,11 @@ def rank_program(g, core, T, topo):
         ins = o["fn"]()
         if j in mark:
             ins.then_inc(T.sem[mark[j][0]], 1 if o["sem"] is None else o["n"])
+    left = {}
     for o in ops:
         if o["sem"] and o["sem"] not in waited:
-            g.sync.wait_ge(T.sem[o["sem"]], o["n"])
+            left[o["sem"]] = left.get(o["sem"], 0) + o["n"]
+    for s, n in left.items():
+        g.sync.wait_ge(T.sem[s], n)
     if sent:
         g.wait_ge(T.sem.sent, sent)

from concourse.bass import DstId, RemoteDMATransfer
from concourse.mybir import AluOpType as ALU, ActivationFunctionType as ACT

V, A, NW = 2560, 64, 160
W, C0 = V + 16, A // 16
XS = 13 * NW
XW = XS // 16
CB = 33280.0
ON_G = (0, 2, 4)
ZS, HS = 1280, 2048
VOTES = [[("s", 320), ("b", V)], [("s", V)], [("v", V)], [("v", V)]]
LATE = {(0, 4): ("b", 1), (1, 1): ("d", 0), (1, 4): ("d", 1), (2, 1): ("nbi", 0), (2, 4): ("nbi", 1)}
PT = [(A, 1056), (1056, V)]
NEW = [(A, 1056), (1056, XS), (XS, V)]
XP = [(A, XS), (XS, V)]
EV = [(A, 1024), (1024, 1536), (1536, 2048), (2048, V)]
OUT = [(0, 1120, "a")] + [(_n, _n + NW, "v") for _n in range(1120, XS, NW)]
CY, GAM, WAKE, LOOK = 0.00083, 1.45, 0.17, 0.05

SCRATCH = {}
for _n in ("b", "d", "PD", "GD", "s", "Hh", "Z", "Zp", "tb", "D0", "D1", "D2", "D3", "U0", "U1", "U2", "U3", "U4"):
    SCRATCH[_n] = ("sbuf", [128, V], "bfloat16")
for _n in ("h", "gs", "P0", "P1", "T1", "T2"):
    SCRATCH[_n] = ("sbuf", [128, W], "bfloat16")
for _n in ("C0", "C1"):
    SCRATCH[_n] = ("sbuf", [128, 5 * V], "bfloat16")
for _n in ("S0", "S1", "SD"):
    SCRATCH[_n] = ("sbuf", [128, W], "float32")
for _n in range(6):
    SCRATCH["L%d" % _n] = ("sbuf", [128, NW], "uint16")
SCRATCH["psW"] = ("psum", [128, V], "float32")
for _n in ("XA", "XB", "XC"):
    SCRATCH["ps" + _n] = ("psum", [128, 512], "float32")
for _n in ("I1", "Im1", "I2", "I256", "I512", "I1024"):
    SCRATCH[_n] = ("sbuf", [128, 128], "bfloat16")
for _n in ("BD", "BE", "BG"):
    SCRATCH[_n] = ("sbuf", [128, 144], "bfloat16")
for _n in ("G1", "Gk", "G2k", "Gmk", "G8k", "GE", "GF", "GFm"):
    SCRATCH[_n] = ("sbuf", [128, 8], "bfloat16")
SCRATCH.update({
    "I32": ("sbuf", [128, 128], "float32"), "xi": ("sbuf", [128, 144], "float32"), "xg": ("sbuf", [128, 8], "float32"),
    "ck": ("sbuf", [128, 5 * 128], "bfloat16"), "cc": ("sbuf", [128, NW], "bfloat16"),
    "ki": ("sbuf", [128, 4], "int32"), "kj": ("sbuf", [128, 4], "int32"), "kf": ("sbuf", [128, 12], "float32"),
    "pb": ("sbuf", [128, NW], "int32"), "hl": ("sbuf", [128, 2 * NW], "bfloat16"),
    "dq": ("sbuf", [128, NW], "bfloat16"), "dw": ("sbuf", [128, NW], "bfloat16"),
    "nbi": ("sbuf", [128, 4 * NW], "int32"), "nbl": ("sbuf", [128, 4 * NW], "uint16"),
    "upi": ("sbuf", [128, 4], "int32"), "upr": ("sbuf", [128, 4], "int32"), "l8": ("sbuf", [128, 32], "uint16"),
    "tu": ("sbuf", [128, 8 * A], "bfloat16"), "z8": ("sbuf", [128, 8 * A], "float32"), "rl": ("sbuf", [128, 16], "uint16"),
    "an": ("sbuf", [128, NW], "bfloat16"), "av": ("sbuf", [128, 256], "bfloat16"), "pen": ("sbuf", [128, 4 * 256], "bfloat16"),
    "best": ("sbuf", [128, 256], "float32"), "bi": ("sbuf", [128, 256], "int32"), "bj": ("sbuf", [128, 256], "int32"),
    "kb": ("sbuf", [128, 256], "bfloat16"), "idx": ("sbuf", [128, NW], "uint16"), "po": ("sbuf", [128, NW], "float32"),
    "low": ("sbuf", [128, 512], "bfloat16"), "tie": ("sbuf", [128, 512], "bfloat16"), "pf": ("sbuf", [128, 128], "float32"),
    "ni": ("sbuf", [128, A], "int32"), "nj": ("sbuf", [128, A], "int32"),
})
for _n in ("ha", "ids", "id1", "id2", "kz"):
    SCRATCH[_n] = ("sbuf", [128, A], "bfloat16")
for _n in ("xb", "xu", "kc"):
    SCRATCH[_n] = ("sbuf", [128, A], "float32")
MW = 2 * A + 8
for _e in range(2):
    for _r in range(3):
        SCRATCH["m%d%d" % (_e, _r)] = ("sbuf", [128, MW], "float32")
for _r in range(3):
    SCRATCH["u%d" % _r] = ("sbuf", [128, 2 * A], "float32")

SEMAPHORES = ["cv", "ca", "ct", "cg", "sent", "upr", "s00"] + ["d%d" % _n for _n in range(90)] + \
    ["m%d%d" % (_e, _r) for _e in range(2) for _r in range(3)]


def calls(g, T, topo, r):
    NR = len(T.cores)
    ops, acc, ndma, sent = [], {}, [0], [0]

    def X(name, a=0, b=None, step=1, rows=None, top=128):
        t = T[name]
        b = t.shape[1] if b is None else b
        if rows is not None:
            ap = t[rows:128:16, a:b]
        else:
            ap = t[0:top, a:b] if step == 1 else t[0:top, a:b:step]
        return (ap, [(name, a, b, rows)], (b - a + step - 1) // step)

    def G(win, off):
        return (win[0].indirect(off[0]), win[1] + off[1], 16 * off[2])

    def size(x):
        return 2 if SCRATCH[x[1][0][0]][2] in ("bfloat16", "uint16") else 4

    def op(q, fn, outs, ins, cost, lat=0.0, sem=None, n=1, wire=0.0, lands=(), adds=False):
        me, deps = len(ops), set()
        for wr, regs in ((False, ins), (True, outs)):
            for x in regs:
                if not isinstance(x, tuple):
                    continue
                for name, a, b, rows in x[1]:
                    w = wr
                    if name.startswith("ps"):
                        a, b, w = a // 512 * 512, -(-b // 512) * 512, not adds
                    keep = []
                    for (a2, b2, rows2, w2, j) in acc.get(name, []):
                        hit = a < b2 and a2 < b and (rows is None or rows2 is None or rows == rows2)
                        if hit and (w or w2) and j != me:
                            deps.add(j)
                        if not (w and rows is None and a <= a2 and b2 <= b):
                            keep.append((a2, b2, rows2, w2, j))
                    acc[name] = keep + [(a, b, rows, w, me)]
        ops.append({"q": q, "fn": fn, "deps": deps, "sem": sem, "n": n, "cost": cost, "lat": lat, "after": set(), "wire": wire, "lands": lands})
        return me

    def val(x):
        return x[0] if isinstance(x, tuple) else x

    def cyc(o, a, per):
        return 0.06 + CY * max(64, o[2] * (GAM if len(a[1]) > 1 else per))

    def dma(q, out, in_):
        k = ndma[0] if out[1] else 89
        ndma[0] += 1
        e = g.sync if q == "s" else g.scalar
        side = out if out[1] else in_
        nbytes = side[2] * size(side) * (128 if side[1][0][3] is None else 8)
        return op(q, lambda: e.dma_start(out[0], in_[0]), [out], [in_], 0.06, 1.3, sem="d%d" % k, n=16, wire=nbytes / 250e3)

    def dram(ap):
        return (ap, [], 0)

    def tt(o, a, b, alu):
        return op("v", lambda: g.vector.tensor_tensor(o[0], a[0], b[0], alu), [o], [a, b], cyc(o, a, 1 if a[1][0][0].startswith("ps") else 2))

    def ts(o, a, s1, s2, o0, o1=None):
        c = cyc(o, a, 0.5 if size(o) + size(a) == 4 else 1)
        if o1 is None:
            return op("v", lambda: g.vector.tensor_scalar(o[0], a[0], val(s1), None, o0), [o], [a, s1], c)
        return op("v", lambda: g.vector.tensor_scalar(o[0], a[0], val(s1), val(s2), o0, o1), [o], [a, s1, s2], c)

    def cp(o, a):
        return op("v", lambda: g.vector.tensor_copy(o[0], a[0]), [o], [a], cyc(o, a, 0.5 if size(o) + size(a) == 4 else 1))

    def fill(o, c):
        return op("v", lambda: g.vector.memset(o[0], c), [o], [], cyc(o, o, size(o) / 4))

    def act(o, a, f=ACT.Identity, bias=0.0, scale=1.0):
        return op("a", lambda: g.scalar.activation(o[0], a[0], f, bias=val(bias), scale=val(scale)), [o], [a, scale, bias], 0.02 + cyc(o, a, 1))

    def gcp(o, a):
        return op("g", lambda: g.affine_select(o[0], a[0], [[1, o[2]]], ALU.is_ge, 0.0, 0, 0), [o], [a], 0.17 + 2 * CY * o[2])

    def iota(name, pattern, step=0, b=None):
        o = X(name, 0, b)
        if SCRATCH[name][2] == "int32":
            return op("g", lambda: g.iota(o[0], pattern, 0, step), [o], [], 0.13 + 2 * CY * o[2])
        return op("g", lambda: g.iota(o[0], pattern, 0, step, allow_small_or_imprecise_dtypes=True), [o], [], 0.13 + 2 * CY * o[2])

    def mms(items, start, stop):
        def fn():
            for n, (o, l, x) in enumerate(items):
                ins = g.tensor.matmul(o[0], l[0], x[0], start and n == 0, stop and n == len(items) - 1)
            return ins
        return op("t", fn, [o for o, l, x in items], [y for o, l, x in items for y in (l, x)],
                  sum(0.01 + CY / 2 * max(min(64, l[2]), x[2]) * size(x) ** 2 / 4 for o, l, x in items), adds=not (start or stop))

    def wrap(bank, n, src, col, base):
        for q in range(0, 16, 4):
            mms([(X(bank, 0, n), X(base, 15 - i, 143 - i), X(src, col + i, col + 16 * n, 16)) for i in range(q, q + 4)], q == 0, q == 12)

    def turn(bank, c0, part, src, col, sel):
        a, b = XP[part]
        for q in range(0, 16, 8):
            mms([(X(bank, c0 + i, c0 + 128, 16, top=(b - a) // 16), X(src, col + a + i, col + b, 16), X(sel)) for i in range(q, q + 8)], False, False)

    def terms(items, start, stop, a0, b0, shift=0):
        cut = [a0] + [c + shift for c in range(512, V, 512) if a0 < c + shift < b0] + [b0]
        for a, b in zip(cut, cut[1:]):
            mms([(X("psW", a - shift, b - shift), X(l), X(x, a, b)) for l, x in items], start, stop)

    def later(k):
        return list(range(k + 1, NR))

    def engines(k, dsts):
        es = [e for e in topo.engines(T.cores[k], T.cores[dsts[0]]) if all(e in topo.engines(T.cores[k], T.cores[x]) for x in dsts)]
        return es if k else es[:len(es) // 2]

    def send(src, land, dsts, lat, dst=None):
        ids = [DstId(rid=topo.addr(T.cores[k])[0], pnc=topo.addr(T.cores[k])[1]) for k in dsts]
        es = engines(r, dsts)
        sent[0] += len(es)
        tr = RemoteDMATransfer(dst_ids=ids, dma_engine_mask=sum(1 << e for e in es), remote_sem=T.sem[land],
                               srcs=[src[0]], dsts=[(dst or src)[0] for _ in dsts])
        return op("g", lambda: g.remote_dma_fused([tr], local_sem=T.sem.sent), [], [src], 0.8 if sent[0] > len(es) else 3.0, lat, sem="",
                  lands=[(k, land) for k in dsts])

    def arrive(x, name, frm, dsts):
        return op("x", None, [x], [], 0.0, sem=name, n=len(engines(frm, dsts)))

    def kf(j):
        return X("kf", j, j + 1)

    def lst(k, a, b):
        return X("L%d" % k, a // 16, b // 16)

    def nbl(k, a, b):
        return X("nbl", k * NW + a // 16, k * NW + b // 16)

    def mklist(k, bank, src, a, b):
        wrap(bank, (b - a) // 16, src, a, "BE")
        return cp(lst(k, a, b), X(bank, 0, (b - a) // 16))

    def twin(dst, src, a, b, j):
        return gcp(X(dst, a, b), X(src, a, b)) if j in ON_G else dma("s", X(dst, a, b), X(src, a, b))

    def pieces(a, b, most):
        n = -((a - b) // most)
        cut = [a + (b - a) * i // n // 32 * 32 for i in range(n)] + [b]
        return list(zip(cut, cut[1:]))

    def line(*lists):
        seq = [x[n] for n in range(max(map(len, lists))) for x in lists if n < len(x)]
        for a, b in zip(seq, seq[1:]):
            ops[b]["after"].add(a)
        return seq

    XB3 = ["psXA", "psXB", "psXC"]
    RB = pieces(A, V, (V - A) // 5 + 32)
    BN = [(max(A, 512 * j), 512 * j + 512) for j in range(5)]
    sends = r < NR - 1

    dma("s", X("pb"), dram(T.par[:]))
    counts = [iota("ki", [[0, 1]], 1, 1), iota("xi", [[1, 144]]), iota("xg", [[16, 8]]), iota("cc", [[1, NW]])]
    if r > 0:
        dma("a", X("upi"), dram(T.up[:]))
        counts.append(send(X("upi"), "upr", [r - 1], 8.0, X("upr")))
        ops[counts[-1]]["after"].update(counts[:-1])
    dma("a", X("ha"), dram(T.hf[:, 0:A]))
    dma("s", X("h", A, HS), dram(T.hf[:, A:HS]))
    ops[iota("ck", [[NW, 5], [0, 128]])]["after"].update(counts)
    fill(X("C0", A, V), 0.0)
    ts(X("kj", 0, 1), X("ki", 0, 1), 15, None, ALU.bitwise_and)
    ts(X("kj", 1, 2), X("ki", 0, 1), 112, None, ALU.bitwise_and)
    cp(kf(0), X("ki", 0, 1))
    cp(X("kf", 1, 3), X("kj", 0, 2))
    ts(X("kf", 5, 8), X("xi", 0, 3), kf(1), None, ALU.is_equal)
    act(kf(4), kf(6), bias=kf(7))
    act(kf(8), kf(5), bias=1.0, scale=-0.75)
    act(kf(9), kf(5), bias=1.0)
    act(kf(10), kf(6), scale=float(V))
    ts(X("hl", 0, NW), X("pb"), 8.0, 0.0, ALU.subtract, ALU.max)
    tt(X("hl", NW, 2 * NW), X("pb"), X("hl", 0, NW), ALU.subtract)
    first = [dma("s", X("C0", 0, V, rows=1), X("hl", 0, NW)), dma("s", X("C0", 0, V, rows=2), X("hl", NW, 2 * NW))]
    first.append(dma("s", X("h", HS, V), dram(T.hf[:, HS:V])))
    ops[first[2]]["deps"].update(ops[first[1]]["deps"])
    late = {}
    for name, src in (("b", T.bt), ("d", T.dr), ("nbi", T.nb)):
        n = T[name].shape[1] // 2
        late[name] = [dma("s", X(name, a, a + n), dram(src[:, a:a + n])) for a in (0, n)]
        ops[late[name][0]]["after"].update(first)
    ops[dma("s", X("dq"), dram(T.dr[0:128:16, :]))]["after"].update(late["d"])
    ts(X("I1"), X("xi", 0, 128), kf(0), None, ALU.is_equal)
    ts(X("BD"), X("xi"), 15.0, kf(2), ALU.subtract, ALU.is_equal)
    ts(X("G1"), X("xg"), kf(2), None, ALU.is_equal)
    for name, src, w in (("BE", "BD", kf(4)), ("BG", "BD", kf(6)), ("GF", "G1", kf(5)),
                         ("I256", "I1", 256.0), ("I2", "I1", 2.0), ("Im1", "I1", -1.0), ("I512", "I1", 512.0), ("I1024", "I1", 1024.0),
                         ("I32", "I1", 1.0), ("Gk", "G1", 1024.0), ("G2k", "G1", 2048.0), ("Gmk", "G1", -1024.0), ("G8k", "G1", 8192.0), ("GE", "G1", kf(4)),
                         ("GFm", "GF", -1.0)):
        act(X(name), X(src), scale=w)
    act(X("id1"), X("xi", 0, A), bias=1.0, scale=kf(6))
    act(X("id2"), X("xi", 0, A), bias=kf(9), scale=kf(6))
    act(X("ids"), X("xi", 0, A), scale=kf(7))
    for name in ("C0", "C1", "T1", "T2"):
        act(X(name, 0, A), X("xi", 0, A), bias=kf(10), scale=0.0)
    for name in ("T1", "T2"):
        act(X(name, V, W), X("xi", 0, 16), bias=kf(10), scale=0.0)
    tt(X("h", 0, A), X("id2"), X("ha"), ALU.mult)
    tt(X("P1", 0, A), X("id1"), X("ha"), ALU.mult)
    gcp(X("P0", 0, A), X("P1", 0, A))
    for name in ("P1", "P0"):
        act(X(name, V, W), X("xi", 0, 16), bias=1.0, scale=0.0)
    for name in ("S0", "S1"):
        gcp(X(name, 0, A), X("b", 0, A))
        act(X(name, V, W), X("xi", 0, 16), scale=0.0)
    spare = [ts(X(name, 0, C0), X("cc", 0, C0), 16.0, kf(1), ALU.mult, ALU.add) for name in ("L0", "idx")]
    if r == 0:
        fill(X("u0", 0, A), 1.0)
        fill(X("kz"), 0.0)
        fill(X("kc"), CB - 127.5)
    made = {(0, part): mklist(0, XB3[part], "C0", a, b) for part, (a, b) in enumerate(PT)}
    ts(X("PD", A, HS), X("h", A, HS), kf(8), None, ALU.mult)
    line([made[0, 0], ts(X("PD", HS, V), X("h", HS, V), kf(8), None, ALU.mult)])
    cp(X("nbl"), X("nbi"))
    if sends:
        arrive(X("upr"), "upr", r + 1, [r])
        cp(X("l8", 0, 4), X("upr"))
    for a, b in pieces(A, V, 900):
        act(X("gs", a, b), X("d", a, b), ACT.Sign, bias=127.5, scale=-1.0)
    act(X("dw"), X("dq"), ACT.Sign, bias=127.5, scale=-1.0)
    act(X("dq"), X("dw"), scale=0.25)
    gcp(X("gs", 0, A), X("id2"))
    act(X("low"), X("ck", 0, 512), bias=-2.0 ** 24, scale=0.0)
    act(X("tie"), X("ck", 0, 512), bias=4096.0, scale=0.0)

    for e in range(2):
        C = "C%d" % e
        TT = [C, "T1", "T2", "T1", "T2"]
        PP = ["h" if e == 0 else "gs", "P1", "P0", "P1", "P0", "P1"]
        SS = ["S0", "S1", "S0", "S1", "S0", "S1"]
        mn = "m%d%d" % (e, r)
        uh = X("u0" if r == 0 else "m%d0" % e if r == 1 else "u%d" % (r - 1), 0, A)

        block, walks = {}, {}
        for k in range(5):
            for j, (a, b) in enumerate(RB if k < 4 else BN):
                n = tt(X(PP[k + 1], a, b), G(X(PP[k], 0, V if k == 0 else W), lst(k, a, b)), X("GD" if k == 0 and e == 1 else "PD", a, b), ALU.mult)
                block[k, j] = n
                if e == 0 and (k, j) in LATE:
                    ops[late[LATE[k, j][0]][LATE[k, j][1]]]["deps"].add(n)
                if k < 4:
                    twin("PD", PP[k + 1], a, b, j)
            for part, (a, b) in enumerate(PT if k < 4 else []):
                jump = act(X(TT[k + 1], a, b), G(X(TT[k], 0, V if k == 0 else W), lst(k, a, b)))
                made[k + 1, part] = mklist(k + 1, XB3[part], TT[k + 1], a, b)
            if sends and 1 <= k < 4:
                n = 2 << k
                act(X("tu", 16 * n, 32 * n), G(X(TT[k + 1]), X("l8", 0, n)))
                wrap("psXC", n, "tu", 16 * n, "BE")
                walks[k] = cp(X("l8", n, 2 * n), X("psXC", 0, n))
        gcp(X(C, 0, A), X("ids"))
        if e == 1:
            spare = [tt(X("D1", a, b), G(X("Hh"), lst(0, a, b)), X("d", a, b), ALU.mult) for a, b in NEW[:2] + [(XS, 2336), (2336, V)]]
            for a, b in EV:
                act(X("Zp", a, b), G(X("Z"), lst(0, a, b)))
        for j, (a, b) in enumerate(EV):
            if e == 0:
                terms([("I1", "b"), ("I256", "h")], True, True, a, b)
                act(X("U0", a, b), X("psW", a, b), ACT.Relu, bias=-256.0)
                terms([("I2", "U0"), ("Im1", "b")], True, False, a, b)
            else:
                terms([("I1", "Z"), ("I512", "gs")], True, False, a, b)
                terms([("I2", "D1")], False, False, a, b)
                terms([("Im1", "Zp")], False, True, a, b)
                n = act(X("SD", a, b), X("psW", a, b), ACT.Abs)
                if j < 2:
                    ops[jump]["after"].add(n)
                terms([("I32", "SD")], True, False, a, b)
        for j, (a, b) in enumerate(BN):
            block["s", j] = ts(X("s", a if j else 0, b), X(PP[5], a if j else 0, b), 0.0, 0.5, ALU.is_gt, ALU.subtract)
            terms([("I512" if e == 0 else "I1024", "s")], False, True, a, b)
            steps = act(X("S0", a, b), X("psW", a, b), ACT.Abs, bias=0.0 if e == 0 else -512.0)
        seq = []
        for k in range(5):
            B = [block[k, j] for j in range(5)]
            seq += B[:1] + ([made[k, 1]] if k or not e else [])
            if k < 4:
                seq += B[1:4] + ([made[k + 1, 0]] if k or not e else []) + B[4:]
                seq += ([spare[0], made[1, 0], spare[1]], spare[2:3], spare[3:], [])[k] if e else spare[k:k + 1]
                seq += [walks[k - 1]] if k - 1 in walks else []
            else:
                seq += [n for j in range(1, 5) for n in (B[j], block["s", j - 1])] + [block["s", 4]]
        line(seq)
        for j, (a, b) in enumerate(RB):
            twin("SD", "S0", a, b, j)
        for a, b in ((0, 2048), (2048, V)):
            dma("s", X(C, a, b, rows=0), X(PP[5], a, b, rows=0))
        if sends:
            ops[act(X("tu", 0, A), G(X(PP[5], 0, V), X("l8", 0, 4)))]["after"].add(steps)
            act(X(mn, 0, A), X("tu", 0, A), ACT.Sign)
            if r == e == 0:
                send(X(mn, 0, A), "s00", later(0), 8.0)
            if r > 0:
                wrap("psXC", 4, "tu", 0, "BG")
                act(X(mn, 2 * A, 2 * A + 4), X("psXC", 0, 4), ACT.Abs)
                act(X(mn, 2 * A + 4, MW), X("psXC", 0, 4), ACT.Abs)
        wrap("psXA", NW, PP[5], 0, "BG")
        act(X("an"), X("psXA", 0, NW), ACT.Abs)
        anchors = ts(X("L5"), X("an"), 1.0, None, ALU.subtract)
        mms([(X("psXB", c, c + 128), X("I1"), X("ck", 0, 128)) for c in (0, 128)], True, False)
        for part in range(2):
            turn("psXB", 128 * part, part, PP[5], 0, "GF")
        mms([(X("psXB", 0, A), X("I1"), X("ck", 0, A))], False, True)
        act(X("av"), X("psXB", 0, 256), ACT.Abs)

        cands = []
        for k in range(4):
            bank = XB3[(k + 2) % 3]
            mms([(X(bank, 0, 256), X("I1"), X("av"))], True, False)
            for a, b in pieces(A, V, 900):
                cands.append(act(X(C, (k + 1) * V + a, (k + 1) * V + b), G(X(C, 0, V), nbl(k, a, b)), ACT.Abs))
            n0 = len(ops)
            for part in range(2):
                turn(bank, 128 * part, part, C, (k + 1) * V, "GFm")
            mms([(X(bank, 0, A), X("I1"), X("ck", 0, A))], False, True)
            pens = range(n0, len(ops))
            act(X("pen", k * 256, k * 256 + 256), X(bank, 0, 256), ACT.Relu, scale=2.0 ** 60)

        sums = {}
        for k in range(5):
            for j, (a, b) in enumerate(RB if k < 4 else BN):
                sums[k, j] = tt(X(SS[k + 1], a, b), G(X(SS[k]), lst(k, a, b)), X("SD", a, b), ALU.add)
                if k < 4:
                    n = twin("SD", SS[k + 1], a, b, 1 if sends and (k, j) == (2, 2) else j)
                    if sends and j in ON_G and (k, j) > (2, 2):
                        ops[n]["after"].add(out)
            if k == 1 and sends:
                far = act(X("z8"), G(X(SS[2]), X("l8")))
                mms([(X("psW", 0, A), X("I32"), X("z8", A * q, A * q + A)) for q in range(8)], True, True)
                line([far, cands[6], act(X(mn, A, 2 * A), X("psW", 0, A))] + cands[7:])
                out = send(X(mn, A if r == e == 0 else 0, MW if r > 0 else 2 * A), mn, later(r), 2.0)
        k = 0 if e or not sends else 1
        line([sums[k, 4], anchors, sums[k + 1, 0]])
        if r > 0:
            if e == 0:
                arrive(X("m00", 0, A), "s00", 0, later(0))
            for k in range(r):
                arrive(X("m%d%d" % (e, k), A if k == e == 0 else 0), "m%d%d" % (e, k), k, later(k))
            cur, n0 = "m%d0" % e, len(ops)
            if r == 1:
                cp(X("ni"), X(cur, A, 2 * A))
            for k in range(1, r):
                msg, nxt = "m%d%d" % (e, k), "u%d" % k
                ts(X("rl", 8 * k - 8, 8 * k), X(msg, 2 * A, MW), 1.0, None, ALU.subtract)
                tt(X(nxt), G(X(cur, 0, A), X("rl", 8 * k - 8, 8 * k)), X(msg, 0, 2 * A), ALU.mult)
                tt(X(nxt, A, 2 * A) if k < r - 1 else X("ni"), G(X(cur, A, 2 * A), X("rl", 8 * k - 8, 8 * k - 4)), X(nxt, A, 2 * A), ALU.add)
                cur = nxt
            act(X("xu"), uh, bias=CB, scale=-127.5)
            ts(X("nj"), X("ni"), 255, None, ALU.bitwise_and)
            tt(X("kz"), X("nj"), uh, ALU.mult)
            tt(X("kc"), X("kz"), X("xu"), ALU.add)
            s = [n for n in range(n0, len(ops)) if ops[n]["q"] == "v"]
            slots = {1: [[], [], s[:1]], 2: [s[:1], s[1:2], s[2:3]], 3: [s[0:4:3], s[1:2], s[2:5:2], s[5:6]]}[r] + [s[-3:-1], s[-1:], []]
            line([n for x, slot in zip(sorted(sums)[17:], slots) for n in [sums[x]] + slot])
        rounded = []
        for j, (a, b) in enumerate(BN):
            a = a if j else 0
            act(X("D0", a, b), G(X("kz"), lst(5, a, b)))
            terms([("I32", "S1")], True, False, a, b)
            terms([("I1", "D0")], False, False, a, b)
            rounded.append(tt(X("tb", a, b), G(X("kc"), lst(5, a, b)), X("S1", a, b), ALU.add))
            terms([("Im1", "tb")], False, True, a, b)
            placed = act(X("Z", a, b), X("psW", a, b), ACT.Abs, bias=CB)
        line(rounded)
        for n in pens:
            ops[n]["after"].add(placed - 1)
        ops[rounded[0]]["after"].update(sums.values())
        if e == 1:
            dma("s", dram(T.yx[:]), X("Z"))
        else:
            ops[dma("s", X("GD", A, V), X("gs", A, V))]["deps"].add(placed)
            dma("s", X("GD", 0, V, rows=0), X("dq"))
            tt(X("xb"), uh, X("b", 0, A), ALU.mult)
            for name in ("P0", "P1"):
                gcp(X(name, 0, A), X("id1"))
            for name in ("S0", "S1"):
                gcp(X(name, 0, A), X("xb"))
            signs = [tt(X("Hh", a, b), G(uh, lst(5, a, b)), X("s", a, b), ALU.mult) for a, b in pieces(0, V, 384)]

        cp(X("Zp", ZS, V), G(X("Z"), lst(0, ZS, V)))
        act(X("Zp", 0, ZS), G(X("Z"), lst(0, 0, ZS)))
        gathers, work, chain = [[], []], [[], []], [[], []]
        for part, (a1, b1) in enumerate(XP):
            four, fifth = (("psXA", "psXB"), ("psXC", "psW"))[part]
            c1, n1, back = 128 * part, (b1 - a1) // 16, 512 + 512 * part
            whole = e == part == 1
            mms([(X(four), X("I1"), X("low" if whole else "ck", 0, 512))] + [(X(four, 128, 512), X("I1"), X("tie", 0, 384))] * whole, True, False)
            for k, ways in enumerate([[("s", V)]] + VOTES):
                if whole and ways[0][0] == "v":
                    ways = [("b", V)]
                D, U, a0 = "D%d" % (k - 1), "U%d" % k, a1
                bank, c0 = (four, 128 * k) if k < 4 else (fifth, 0)
                if k == 4:
                    mms([(X(fifth, 0, 128), X("I1"), x) for x in ([X("low", 0, 128), X("tie", 0, 128)] if whole else [X("ck", 512, 640)])], True, False)
                if whole:
                    turn(bank, c0, part, C, k * V, "GE")
                for way, b0 in ways:
                    b0 = min(b0, b1)
                    if b0 <= a0:
                        continue
                    for a, b in pieces(a0, b0, 1400):
                        if way != "s":
                            work[part].append(tt(X(D, a, b), G(X("Zp"), nbl(k - 1, a, b)), X("Z", a, b), ALU.subtract))
                            gathers[part].append(work[part][-1])
                        elif k > 0:
                            gathers[part].append(act(X(D, a, b), G(X("Zp"), nbl(k - 1, a, b))))
                        if way == "b":
                            act(X(U, a, b), X(D, a, b), ACT.Abs)
                    if way == "v":
                        turn(bank, c0, part, D, 0, "Gmk")
                        work[part].append(ts(X(U, a0, b0), X(D, a0, b0), 0.0, None, ALU.max))
                    for a, b in [(a, min(a + 1024, b0)) for a in range(a0, b0, 1024)] if way == "s" else []:
                        terms([("Im1", "Z")], True, False, a, b, A)
                        terms([("I1", D if k > 0 else "Zp")], False, True, a, b, A)
                        act(X(U, a, b), X("psW", a - A, b - A), ACT.Abs)
                    a0 = b0
                turn(bank, c0, part, U, 0, "G8k" if whole else "G2k" if ways[0][0] == "v" else "Gk")
                if k >= 3:
                    mms([(X(bank, 128 * q % 512, 128 * q % 512 + 128), X("I1"), X("pen", 256 * q - 256 + c1, 256 * q - 128 + c1))
                         for q in ((1, 2, 3) if k == 3 else (4,))], False, True)
            act(X("best", c1, c1 + 128), X(four, 0, 128))
            for k in range(1, 5) if whole else []:
                chain[part].append(tt(X("bi", c1, c1 + 128), X(four, 128 * k, 128 * k + 128) if k < 4 else X(fifth, 0, 128),
                                      X("bj" if k > 1 else "best", c1, c1 + 128), ALU.min))
                chain[part].append(ts(X("bj", c1, c1 + 128), X("bi", c1, c1 + 128), -4097 if k < 4 else 4095, None, ALU.bitwise_and))
            if whole:
                chain[part].append(cp(X("pf"), X("bj", c1, c1 + 128)))
                for q in range(8):
                    dma("sa"[q % 2], dram(T.yp[q, XS:V]), X("pf", 16 * q, 16 * q + 16, top=n1))
                continue
            for k in range(1, 5):
                chain[part].append(tt(X("best" if k < 4 else "bi", c1, c1 + 128), X(four, 128 * k, 128 * k + 128) if k < 4 else X(fifth, 0, 128),
                                      X("best", c1, c1 + 128), ALU.min))
            chain[part].append(ts(X("bj", c1, c1 + 128), X("bi", c1, c1 + 128), 1023, None, ALU.bitwise_and))
            chain[part].append(cp(X("kb", c1, c1 + 128), X("bj", c1, c1 + 128)))
            o = X("psW", back, back + n1)
            mms([(o, X("I1"), X("cc", a1 // 16, b1 // 16))], True, False)
            mms([(o, X("kb", c1, c1 + 128, top=n1), X("I1", 0, n1, top=n1))], False, True)
            chain[part].append(ts(X("idx", a1 // 16, b1 // 16), o, 16.0, kf(1), ALU.mult, ALU.add))
        for n in gathers[1]:
            ops[n]["after"].update(gathers[0])
        ops[line(chain[0][:6], work[1][2:])[0]]["after"].update(work[0] + work[1][:2])
        one = line([chain[0][5], signs[3] if e == 0 else chain[1][0], chain[0][6]])
        if e == 0:
            two = line(chain[1], signs[4:])
            for n, (a, b) in enumerate(NEW):
                act(X("C1", a, b), G(X(C), X("idx", a // 16, b // 16)))
                mklist(0, XB3[n], "C1", a, b)
        else:
            outs = []
            for a, b, q in OUT:
                n = (cp if q == "v" else act)(X("T2", a, b), G(X(C), X("idx", a // 16, b // 16)))
                outs += [n] if q == "v" else []
                mms([(X("psXA", 0, XW), X("BE", 15 - i, 143 - i), X("T2", XW * i, XW * i + XW)) for i in range(a // XW, b // XW)], a == 0, b == XS)
            two = line(outs, chain[1][1:])
            act(X("po", 0, XW), X("psXA", 0, XW))
            dma("s", dram(T.yp[:, 0:XS]), X("po", 0, XW))
        ops[two[0]]["after"].add(one[-1])
    return ops, sent[0]


def gap(ops, a, b):
    return 0.0 if ops[a]["q"] == ops[b]["q"] == "t" or a in ops[b]["soft"] or b in ops[a]["soft"] else WAKE


def arrange(ops, pre, succ, weight, back):
    free, done, count, order = {}, {}, [len(p) for p in pre], []
    ready = {j: ops[j]["lat"] * back for j, p in enumerate(pre) if not p}
    while ready:
        start = {j: max(t, free.get(ops[j]["Q"], 0.0)) for j, t in ready.items()}
        j0 = min(start, key=lambda j: (start[j], -weight[j]))
        j = max((x for x in start if ops[x]["Q"] == ops[j0]["Q"] and start[x] <= start[j0] + LOOK), key=lambda x: weight[x])
        o = ops[j]
        free[o["Q"]] = done[j] = start[j] + o["cost"]
        if o["wire"]:
            free[o["Q"][0]] = done[j] = max(free.get(o["Q"][0], 0.0), done[j]) + o["wire"]
        done[j] += o["lat"] * (1 - back)
        order.append(j)
        del ready[j]
        for s in succ[j]:
            count[s] -= 1
            if count[s] == 0:
                ready[s] = ops[s]["lat"] * back + max(done[d] + gap(ops, d, s) for d in pre[s])
    return order, done


def place(ops, pre, succ, weight, back):
    busy, start, done, count = {}, {}, {}, [len(p) for p in pre]
    ready = {j for j, p in enumerate(pre) if not p}

    def fit(q, t, c):
        line = busy.setdefault(q, [])
        for n, (a, b) in enumerate(line + [(1e9, 1e9)]):
            if t + c <= a + 1e-9:
                break
            t = max(t, b)
        line.insert(n, (t, t + c))
        return t

    while ready:
        j = max(ready, key=lambda x: (weight[x], -x))
        ready.remove(j)
        o = ops[j]
        t = o["lat"] * back + max([done[d] + gap(ops, d, j) for d in pre[j]], default=0.0)
        if o["wire"] and back:
            t = fit(o["Q"][0], t, o["wire"]) + o["wire"]
        start[j] = fit(o["Q"], t, o["cost"])
        done[j] = start[j] + o["cost"]
        if o["wire"] and not back:
            done[j] = fit(o["Q"][0], done[j], o["wire"]) + o["wire"]
        done[j] += o["lat"] * (1 - back)
        for s in succ[j]:
            count[s] -= 1
            if count[s] == 0:
                ready.add(s)
    return sorted(start, key=lambda x: (start[x], done[x])), done


ORDER = {}


def orders(g, T, topo):
    if not ORDER:
        ops, pre, home = [], [], []
        for k in range(len(T.cores)):
            base = len(ops)
            for j, o in enumerate(calls(g, T, topo, k)[0]):
                ops.append(dict(o, Q=(k, o["q"]), soft={base + d for d in o["after"] - o["deps"]}))
                pre.append({base + d for d in o["deps"] | o["after"]})
                home.append((k, j))
        landing = {(o["Q"][0], o["sem"]): j for j, o in enumerate(ops) if o["q"] == "x"}
        for j, o in enumerate(ops):
            for x in o["lands"]:
                pre[landing[x]].add(j)
        succ = [set() for _ in pre]
        for j, p in enumerate(pre):
            for d in p:
                succ[d].add(j)
        order, head = arrange(ops, pre, succ, [-j for k, j in home], 0)
        for rule in (arrange, arrange, place, place, place):
            order, tail = rule(ops, succ, pre, head, 1)
            order, head = rule(ops, pre, succ, tail, 0)
        for j in order:
            ORDER.setdefault(home[j][0], []).append(home[j][1])
    return ORDER


def rank_program(g, core, T, topo):
    r = T.rank_of(core)
    if r is None:
        return
    order = orders(g, T, topo)[r]
    ops, sent = calls(g, T, topo, r)
    Q = {"v": g.vector, "a": g.scalar, "t": g.tensor, "g": g, "s": g.sync}
    CS = {"v": "cv", "a": "ca", "t": "ct", "g": "cg"}
    at = {j: n for n, j in enumerate(order)}
    need = set()
    for o in ops:
        o["deps"] = {d for d in o["deps"] if not (o["q"] == "t" and ops[d]["q"] == "t")}
        last = {}
        for d in o["deps"]:
            if ops[d]["sem"] is None:
                last[ops[d]["q"]] = max(last.get(ops[d]["q"], d), d, key=lambda x: at[x])
        need.update(last.values())
    cnt, mark = {q: 0 for q in CS}, {}
    for j in order:
        o = ops[j]
        if o["sem"] is None:
            if j in need:
                cnt[o["q"]] += 1
                mark[j] = (CS[o["q"]], cnt[o["q"]])
        elif o["sem"]:
            mark[j] = (o["sem"], o["n"])
    seen, waited = {q: {} for q in Q}, set()
    for j in order:
        o = ops[j]
        if o["q"] == "x":
            continue
        want = {}
        for d in o["deps"]:
            if d in mark:
                want[mark[d][0]] = max(want.get(mark[d][0], 0), mark[d][1])
        for s, n in want.items():
            if seen[o["q"]].get(s, 0) < n:
                Q[o["q"]].wait_ge(T.sem[s], n)
                seen[o["q"]][s] = n
                waited.add(s)
        ins = o["fn"]()
        if j in mark:
            ins.then_inc(T.sem[mark[j][0]], 1 if o["sem"] is None else o["n"])
    left = {}
    for o in ops:
        if o["sem"] and o["sem"] not in waited:
            left[o["sem"]] = left.get(o["sem"], 0) + o["n"]
    for s, n in left.items():
        g.sync.wait_ge(T.sem[s], n)
    if sent:
        g.wait_ge(T.sem.sent, sent)
